import numpy as np, ml_dtypes
CORES = [9,25,41,57]
N = 4
BF = ml_dtypes.bfloat16
def gentries(a):
    return np.ascontiguousarray(a.reshape(8, 16, -1).transpose(0, 2, 1)).reshape(8, -1)
def gtable(e):
    e = np.asarray(e); return np.ascontiguousarray(e.reshape(8, -1, 16).transpose(0, 2, 1)).reshape(128, -1).astype(np.int32)
W, L, S, ST = 4096, 256, 16, 5
def parts(rng):
    x = rng.integers(0, 64, (N, 8, 16, W)); v = rng.integers(0, W, (N, 8, L, S)); c = rng.integers(0, W, (N, 8, L, S))
    n = np.where(rng.random((N, 8, L)) < 0.4, rng.integers(0, 4, (N, 8, L)), rng.integers(4, S + 1, (N, 8, L)))
    return x, v, c, n, rng.integers(220, 460, (N, 8)), rng.integers(0, 256, (N, 8, 16))
def pack(x, v, c, n, th, w):
    return {"xc": np.ascontiguousarray(x.reshape(N, 128, W)).astype(np.float32).astype(BF), "vl": np.stack([gtable(a.reshape(8, -1)) for a in v]), "cl": np.stack([gtable(a.reshape(8, -1)) for a in c]),
            "ln": np.ascontiguousarray(n).astype(np.int32), "th": np.ascontiguousarray(th.reshape(N, 8, 1)).astype(np.int32), "wt": np.ascontiguousarray(w.reshape(N, 128, 1)).astype(np.int32)}
def setup_inputs(rng):
    return pack(*parts(rng))
def setup_inputs_ties(rng):
    x, v, c, n, th, w = parts(rng)
    x = np.repeat(8 * rng.integers(0, 8, (N, 8, 1, W)), 16, axis=2); up = rng.integers(0, 3, (N, 8, W)) * (rng.random((N, 8, W)) < 0.4)
    x = x + up[:, :, None, :] * (np.arange(16)[:, None] == rng.integers(0, 16, (N, 8, 1, W)))
    o = np.argsort(rng.random((N, 8)), axis=1); j = o >> 1; less = np.where(rng.random((N, 8)) < 0.6, rng.integers(0, 2, (N, 8)), rng.integers(0, 32, (N, 8)))
    th = np.maximum(128 * j - less, 0); s = np.arange(S)
    for r in range(N):
        z = 128 * int(rng.integers(4, 7))
        for g, e in ((int(np.argmin(o[r])), 0), (int(np.argmax(o[r])), 1)):
            th[r, g] = z + e
            x[r, g, :, 0] = 0; x[r, g, :, 1] = 56; x[r, g, :, 2] = z >> 4; x[r, g, int(rng.integers(0, 16)), 2] += 1
            v[r, g, 1::2] = np.where(s < 2, 0, 2); c[r, g, 1::2] = np.where(s < 1, 1, 2); n[r, g, 1::2] = rng.integers(4, S + 1, L // 2)
    q = int(rng.integers(0, N)); a = (q - 1) % N; b = (q - 2) % N
    n[a] = np.where(n[a] >= 4, rng.integers(4, 6, (8, L)), n[a])
    n[q] = rng.integers(0, 4, (8, L)); p = rng.permutation(8 * L)[:31]; one = rng.integers(0, W, (31, 1))
    n[q, p // L, p % L] = 4; v[q, p // L, p % L] = one; c[q, p // L, p % L] = one; th[q] = 128 * rng.integers(1, 4, 8) - 16
    x[b, :, :, 16:40:3] = 0; x[b, :, :, 17:40:3] = 56; x[b, :, :, 18:40:3] = 63; x[b, :, :, 64:128] = 8 * rng.integers(0, 2, (8, 1, 64))
    f0 = 16 + 3 * (np.arange(L // 4)[:, None] & 7); far = rng.integers(64, 128, (8, L // 4, S)); e = rng.integers(128, W, (8, L // 4, S))
    v[b, :, ::4] = np.where(s == 0, e, np.where((s == 1) | (s >= S - 3), f0 + 2, np.where(s == 2, f0 + 1, far)))
    c[b, :, ::4] = np.where(s == 0, f0 + 2, np.where((s == 1) | (s == S - 3), f0, rng.integers(128, W, far.shape)))
    n[b, :, ::4] = S
    return pack(x, v, c, n, th, w)
def setup_inputs_alike(rng):
    x, v, c, n, th, w = parts(rng)
    few = np.array([0, W - 1, W // 2, 3, W - 2, 17])
    v[:, ::2] = few[rng.integers(0, 6, (N, 4, L, S))]; v[:, 1::2, :, 0] = few[rng.integers(0, 6, (N, 4, L))]
    w[:, ::2] = 0; th[:, ::2] = rng.integers(0, 260, (N, 4)); th[:, 1::2] = rng.integers(150, 500, (N, 4))
    o = rng.permutation(4); shutting = 2 * int(o[0]); taking = 2 * int(o[1]); growing = 1 + 2 * int(rng.integers(0, 4))
    n[:, growing] = rng.integers(4, S + 1, (N, L)); v[:, growing, :, 0] = few[int(rng.integers(0, 6))]; th[:, growing] = 0
    n[:, shutting] = rng.integers(ST + 3, S + 1, (N, L)); th[:, shutting] = 1008
    rest = np.where(rng.random((N, L)) < 0.8, 0, rng.integers(1, 4, (N, L)))
    n[:, taking] = np.where(np.arange(N)[:, None] % 2 == 0, rng.integers(ST + 3, S + 1, (N, L)), rest); th[:, taking] = 1008
    return pack(x, v, c, n, th, w)
def setup_inputs_corners(rng):
    x, v, c, n, th, w = parts(rng)
    lo = (W - 1) * rng.integers(0, 2, (N, 8, 1)); hi = W - 1 - lo
    x[..., 0] = np.where(lo == 0, 0, 63); x[..., W - 1] = np.where(lo == 0, 63, 0)
    n = rng.choice(np.array([0, 1, 2, 3, 4, 5, S - 1, S]), (N, 8, L)); kind = rng.integers(0, 5, (N, 8, L))
    for g, i in ((0, 0), (7, L - 1)):
        n[0, g, i] = S; kind[0, g, i] = 0; n[1, g, i] = 0
    n[N - 1, 7, L - 2] = S; kind[N - 1, 7, L - 2] = 1
    s = np.arange(S); q = np.maximum(n, 4)[..., None]; kd = kind[..., None]; A = lo[..., None]; H = hi[..., None]
    v0 = np.where((s < 2) | (s == q - 1), H, A); v1 = np.where((s == q - 3) | (s == q - 2), H, A); v2 = np.where(s >= q - 3, H, A)
    one = rng.integers(0, W, (N, 8, L, 1))
    v = np.where(kd == 0, v0, np.where(kd == 1, v1, np.where(kd == 2, v2, np.where(kd == 3, one, v))))
    c = np.where(kd < 3, A, np.where(kd == 3, one, c))
    v = np.where(s < n[..., None], v, (W - 1) * rng.integers(0, 2, v.shape)); c = np.where(s < n[..., None], c, (W - 1) * rng.integers(0, 2, c.shape))
    return pack(x, v, c, n, np.array([0, 5, 500, 900])[np.argsort(rng.random((N, 8)), axis=1) >> 1], w)
def setup_inputs_ends(rng):
    x, v, c, n, th, w = parts(rng)
    e = 63 * rng.integers(0, 2, (N, 8, 1)); e[N - 1, 7] = 0
    x = 63 * rng.integers(0, 2, (N, 8, 16, W)); x[..., 0] = e; x[..., W - 1] = 63 - e
    for j in range(1, 17):
        for col in (j, W - 1 - j):
            x[..., col] = 63 - e; x[:, :, j - 1, col] = np.abs(62 - e[..., 0])
    v = np.where(rng.random(v.shape) < 0.75, (W - 1) * rng.integers(0, 2, v.shape), v); c = np.where(rng.random(c.shape) < 0.75, (W - 1) * rng.integers(0, 2, c.shape), c)
    kind = rng.integers(0, 3, (N, 8, L)); kind[..., 0] = 1; kind[..., L - 1] = 1; kind[..., 1] = 2; kind[..., L - 2] = 2
    k1 = kind == 1; k2 = kind == 2; v[k1 | k2] = W - 1; c[k1] = W - 1
    c = np.where(k2[..., None], (W - 1) * rng.integers(0, 2, c.shape), c)
    near = rng.integers(1, 17, (N, 8, L)); near = np.where(rng.random((N, 8, L)) < 0.5, near, W - 1 - near)
    v[..., 0] = np.where(k1, near, v[..., 0]); c[..., 0] = np.where(k1, 0, c[..., 0]); c[..., S - 3] = np.where(k1 | k2, 0, c[..., S - 3])
    v[..., S - 1] = np.where(k1, (W - 1) * rng.integers(0, 2, (N, 8, L)), v[..., S - 1]); v[N - 1, 7, L - 1, S - 1] = 0
    n = np.where(rng.random((N, 8, L)) < 0.7, S, 0); n[..., 0] = S; n[..., 1] = S; n[..., 2] = 0; n[..., L - 2] = S; n[..., L - 1] = S; n[0, :, L - 1] = 0
    th = 1008 * (np.argsort(rng.random((N, 8)), axis=1) & 1)
    if th[N - 1, 7] > 0: th[N - 1] = 1008 - th[N - 1]
    w = 255 * rng.integers(0, 2, (N, 8, 16)); w[:, 7] = 255; w[:, 0] = 0
    return pack(x, v, c, n, th, w)
def setup_inputs_spread(rng):
    x, v, c, n, th, w = parts(rng)
    x = np.minimum((np.exp2(6.1 * rng.random((N, 8, 1, W))) * rng.random((N, 8, 16, W))).astype(np.int64), 63)
    po = rng.choice(np.array([1.0, 2.0, 4.0]), (N, 8, 1, 1)); v = np.minimum((W * rng.random(v.shape) ** po).astype(np.int64), W - 1); c = np.minimum((W * rng.random(c.shape) ** po[:, ::-1]).astype(np.int64), W - 1)
    n = np.minimum(((S + 1) * rng.random((N, 8, L)) ** rng.choice(np.array([0.5, 1.0, 2.0]), (N, 8, 1))).astype(np.int64), S)
    th = np.minimum(np.exp2(10 * rng.random((N, 8))).astype(np.int64) - 1, 1008); w = np.minimum(np.exp2(8.05 * rng.random((N, 8, 16))).astype(np.int64) - 1, 255)
    return pack(x, v, c, n, th, w)
def check_inputs(d):
    bad = []
    for k, lo, hi in (("xc", 0, 63), ("vl", 0, W - 1), ("cl", 0, W - 1), ("ln", 0, S), ("th", 0, 1008), ("wt", 0, 255)):
        a = np.asarray(d[k]).astype(np.float64)
        if not (np.min(a) >= lo and np.max(a) <= hi): bad.append("range of " + k)
    a = np.asarray(d["xc"]).astype(np.float64)
    if not np.all(np.floor(a) == a): bad.append("xc is not whole")
    return bad
def reference(xc, vl, cl, ln, th, wt):
    X = np.ascontiguousarray(xc.astype(np.float32).astype(np.int32).reshape(N, 8, 16, W).transpose(0, 1, 3, 2))
    V = np.stack([gentries(q) for q in vl]).astype(np.int32).reshape(N, 8, L, S); C = np.stack([gentries(q) for q in cl]).astype(np.int32).reshape(N, 8, L, S)
    n = ln.astype(np.int64).reshape(N, 8, L); lim = th.astype(np.int64).reshape(N, 8, 1, 1); w = wt.astype(np.int64).reshape(N, 8, 1, 16)
    a = np.arange(N)[:, None, None, None]; b = np.arange(8)[None, :, None, None]; s = np.arange(S); shut = np.zeros(N, np.int64)
    for t in range(ST):
        XV = X[a, b, V]; XC = X[a, b, C]; live = n >= 4
        bend = np.add.reduce(np.abs(XV[:, :, :, :-1] + XV[:, :, :, 1:] - 2 * XC[:, :, :, :-1]), axis=-1, dtype=np.int32)
        k = np.argmax(np.where(s[:-1] <= n[..., None] - 3, bend, -1), axis=3)[..., None]
        Vk = np.take_along_axis(V, k, 3); Vn = np.take_along_axis(V, k + 1, 3); Ck = np.take_along_axis(C, k, 3)
        y = np.clip(X[a, b, Vk] + X[a, b, Vn] - X[a, b, Ck], 0, 63)
        dist = np.add.reduce(np.abs(XV - y), axis=-1, dtype=np.int32)
        fit = (s >= k + 2) & (s <= n[..., None] - 1) & (dist <= lim + shut[:, None, None, None]) & live[..., None]
        close = np.any(fit, axis=3); m = np.argmax(fit, axis=3)[..., None]; grow = live & ~close
        size = np.where(close[..., None], m - k - 1, 0)
        ix = np.minimum(k + 1 + s, S - 1); keep = s < size
        PV = np.where(keep, np.take_along_axis(V, ix, 3), 0); PC = np.where(keep, np.take_along_axis(C, ix, 3), 0)
        y = y[:, :, :, 0]; u = np.add.reduce(w * y, axis=-1) & (W - 1)
        h = (((u * u) >> 5) + 37 * Vk[..., 0].astype(np.int64)) & (W - 1)
        src = np.minimum(np.where(s <= k, s, s + size - grow[..., None].astype(np.int64)), S - 1)
        V2 = np.take_along_axis(V, src, 3); C2 = np.take_along_axis(C, src, 3); new = grow[..., None] & (s == k + 1)
        V2 = np.where(new, h[..., None], V2); C2 = np.where(new, Vk, np.where(live[..., None] & (s == k), Vn, C2))
        n2 = np.minimum(n + grow.astype(np.int64), S) - size[..., 0]
        for i in range(L - 1, -1, -1):
            p, q = np.nonzero(grow[:, :, i]); X[p, q, h[p, q, i]] = y[p, q, i]
        d = 1 + t % (N - 1)
        came = np.roll(size, d, axis=0)[..., 0]; yin = np.roll(y, d, axis=0); lin = np.roll(live, d, axis=0)
        take = ~live & (came > n)
        V = np.where(take[..., None], np.roll(PV, d, axis=0), V2); C = np.where(take[..., None], np.roll(PC, d, axis=0), C2); n = np.where(take, came, n2)
        V = np.where(s < n[..., None], V, 0).astype(np.int32); C = np.where(s < n[..., None], C, 0).astype(np.int32)
        has = lin & (n >= 1); old = X.copy()
        for i in range(L - 1, -1, -1):
            p, q = np.nonzero(has[:, :, i]); z = V[p, q, i, 0]; X[p, q, z] = (old[p, q, z] + yin[p, q, i]) >> 1
        shut = np.add.reduce(close.astype(np.int64).reshape(N, -1), axis=1) & 31
    return {"yx": np.ascontiguousarray(X.transpose(0, 1, 3, 2)).reshape(N, 128, W).astype(np.float32).astype(BF), "yv": np.stack([gtable(q.reshape(8, -1)) for q in V]).astype(np.float32),
            "yc": np.stack([gtable(q.reshape(8, -1)) for q in C]).astype(np.float32), "yn": n.astype(np.float32)}

@@ -1,0 +1,633 @@
+from concourse.mybir import AluOpType, AxisListType, ActivationFunctionType
+
+OP = AluOpType
+AF = ActivationFunctionType
+W, L, S, ST = 4096, 256, 16, 5
+BIG = 8388608.0
+F32, BF, I32, U16 = "float32", "bfloat16", "int32", "uint16"
+
+MEASURE = ("gc0 ss0 masks gv1 ss1 dd0 ab0 ky0 pk0 gc1 dd1 gv2 ee0 ab1 ss2 ky1 ae0 gc2 dd2 gv3 ab2 ds0 gc3 "
+           "pk1 ky2 ee1 ss3 pk2 ee2 ae1 dd3 ab3 ae2 ky3 ds1 ds2 pk3")
+SCRATCH = {"X": ("sbuf", [128, W + L], BF)}
+ALIAS = {}
+
+
+def _pack(buf, names, cols, d):
+    names = names.split()
+    for k, n in enumerate(names):
+        ALIAS[n] = (buf, k * cols, cols, d)
+    SCRATCH[buf] = ("sbuf", [128, len(names) * cols], d)
+
+
+def _add(names, cols, d):
+    for n in names.split():
+        SCRATCH[n] = ("sbuf", [128, cols], d)
+
+
+for _c in range(4):
+    _add("GV%d SS%d GC%d" % (_c, _c, _c), 1024, BF)
+_add("AB0 AB1 EE0 EE1 AE0 AE1", 1024, BF)
+_add("V N C VCB CIN2 CT1 CT2 DG", 256, F32)
+_pack("MF", "PW m1 m2 m3 m4 m5 m6 m7 m8 m9 KS LM RS MP CT3 QC Hx f1 f2 SO VCA kb s6B zb xB NKB VKB TKb kthB mthB MXB kqB ngB nlB KVs", 256, F32)
+_add("SK SM IV IC iw LNI", 256, I32)
+_add("Pb Vg VL B3 Y Yn SYs GYs BL BL2 Pa Pr g1 g2", 256, BF)
+_add("LST", 768, U16)
+_add("Ru", 256, U16)
+_add("EQ", 2176, BF)
+_pack("PLF", "nn V0 live kq kp2 VK NK ng nl close grow gsel rest MXe TR hm hp cnt s1 s2 s3 s4 s5 s6 s7 s8 s9 zL take kqe mth kth x", 16, F32)
+_pack("PLI", "KA KB UI HI K37 MX VM", 16, I32)
+_pack("PLU", "o16 off16 z16 bcA bc15", 16, U16)
+_add("bcY", 64, U16)
+_pack("COF", "pcF pmF p4F btF thm lim cs1 e1 e2 wF ws", 1, F32)
+_pack("COI", "pcI pmI p4I btI cI", 1, I32)
+_add("WI THI", 1, I32)
+_add("mq mg mm blkF onesF G8", 128, F32)
+_pack("IDS", "Ident In1 In2 Ibig Im256 Im4k ones blk blk8k", 128, BF)
+_add("LQ1 LQk LW", 2048, BF)
+_add("CR", 64, BF)
+_add("cc", 64, F32)
+_add("LNF THF", 256, F32)
+_add("G8T", 8, F32)
+_add("bcI", 64, I32)
+for _t in range(ST):
+    _add("rL%d" % _t, 768, U16)
+    _add("rP%d rY%d" % (_t, _t), 256, BF)
+    _add("rB%d" % _t, 48, F32)
+_add("SB", 48, F32)
+for _b in range(8):
+    SCRATCH["pb%d" % _b] = ("psum", [128, 512], F32)
+
+SEMAPHORES = ["sV", "sS", "sT", "sG", "lR", "lP", "lY", "lB"]
+SEMAPHORES += ["a%s%d" % (m, t) for m in "RPYB" for t in range(ST)]
+SEMAPHORES += ["d%d" % k for k in range(24)]
+
+
+def rank_program(g, core, T, topo):
+    rank = T.rank_of(core)
+    if rank is None:
+        return
+    queues = {"V": g.vector, "S": g.scalar, "T": g.tensor, "G": g, "Y": g.sync}
+    count = {}
+    known = {q: {} for q in queues}
+    clock = {}
+    recs = {}
+    ndma = [0]
+
+    def v(name, lo=0, hi=None, step=1, p=None):
+        if name in ALIAS:
+            name, at, width, _d = ALIAS[name]
+            hi = at + (width if hi is None else hi)
+            lo += at
+        hi = SCRATCH[name][1][1] if hi is None else hi
+        t = T[name]
+        sl = slice(lo, hi, step) if step != 1 else slice(lo, hi)
+        return (t[:, sl] if p is None else t[0:p, sl], [(name, lo, hi)])
+
+    def ind(win, off):
+        return (win[0].indirect(off[0]), win[1] + off[1])
+
+    def need(q, reads, writes):
+        toks = []
+        for acc, wr in [(a, False) for a in reads] + [(a, True) for a in writes]:
+            name, lo, hi = acc
+            bank = name.startswith("pb")
+            for (l2, h2, tok, q2, w2) in recs.get(name, []):
+                if bank and q2 != q:
+                    toks.append(tok)
+                elif lo < h2 and l2 < hi and (wr or w2):
+                    if q2 == q and q == "T":
+                        continue
+                    toks.append(tok)
+        return toks
+
+    def wait(q, toks):
+        best = {}
+        for s, n in toks:
+            best[s] = max(best.get(s, 0), n)
+        kn = known[q]
+        todo = sorted(best.items(), key=lambda a: -len(clock.get(a, {})))
+        for s, n in todo:
+            if kn.get(s, 0) >= n:
+                continue
+            if any(clock.get((s2, n2), {}).get(s, 0) >= n for s2, n2 in todo if s2 != s and kn.get(s2, 0) < n2):
+                continue
+            queues[q].wait_ge(T.sem[s], n)
+            for s3, n3 in clock.get((s, n), {}).items():
+                kn[s3] = max(kn.get(s3, 0), n3)
+            kn[s] = max(kn.get(s, 0), n)
+
+    def record(q, tok, reads, writes):
+        for acc, wr in [(a, False) for a in reads] + [(a, True) for a in writes]:
+            name, lo, hi = acc
+            old = recs.get(name, [])
+            if name.startswith("pb"):
+                old = [r for r in old if r[3] == q]
+            if wr:
+                old = [r for r in old if not (lo <= r[0] and r[1] <= hi)]
+            else:
+                old = [r for r in old if r[4] or r[3] != q or (r[0], r[1]) != (lo, hi)]
+            old.append((lo, hi, tok, q, wr))
+            recs[name] = old
+
+    def bump(q, sem, n):
+        count[sem] = count.get(sem, 0) + n
+        tok = (sem, count[sem])
+        clock[tok] = dict(known[q])
+        return tok
+
+    def op(q, fn, reads, writes):
+        rd = [a for x in reads for a in x[1]]
+        wr = [a for x in writes for a in x[1]]
+        wait(q, need(q, rd, wr))
+        inst = fn(queues[q])
+        sem = "s" + q
+        inst.then_inc(T.sem[sem], 1)
+        record(q, bump(q, sem, 1), rd, wr)
+
+    def dma(q, out, in_, reads=(), writes=()):
+        rd = [a for x in reads for a in x[1]]
+        wr = [a for x in writes for a in x[1]]
+        wait(q, need(q, rd, wr))
+        sem = "d%d" % ndma[0]
+        ndma[0] += 1
+        queues[q].dma_start(out, in_).then_inc(T.sem[sem], 16)
+        record(q + "d", bump(q, sem, 16), rd, wr)
+
+    def tt(out, a, b, o):
+        op("V", lambda e: e.tensor_tensor(out[0], a[0], b[0], o), [a, b], [out])
+
+    def ts(out, a, s1, o0, s2=None, o1=None):
+        rd = [a] + [x for x in (s1, s2) if isinstance(x, tuple)]
+        x1 = s1[0] if isinstance(s1, tuple) else s1
+        x2 = s2[0] if isinstance(s2, tuple) else s2
+        if o1 is None:
+            op("V", lambda e: e.tensor_scalar(out[0], a[0], x1, None, o0), rd, [out])
+        else:
+            op("V", lambda e: e.tensor_scalar(out[0], a[0], x1, x2, o0, o1), rd, [out])
+
+    def cp(out, a):
+        op("V", lambda e: e.tensor_copy(out[0], a[0]), [a], [out])
+
+    def act(out, a, f=AF.Copy, scale=1.0, bias=0.0):
+        op("S", lambda e: e.activation(out[0], a[0], f, bias=bias, scale=scale), [a], [out])
+
+    def mm(out, l, r, start, stop):
+        op("T", lambda e: e.matmul(out[0], l[0], r[0], start, stop), [l, r], [out])
+
+    def scan(out, d0, d1, o0, o1):
+        op("V", lambda e: e.tensor_tensor_scan(out[0], d0[0], d1[0], 0.0, o0, o1), [d0, d1], [out])
+
+    def tr(out, a):
+        op("V", lambda e: e.transpose(out[0], a[0]), [a], [out])
+
+    def fill(out, c):
+        op("V", lambda e: e.memset(out[0], c), [], [out])
+
+    def iota(out, pat, base, cm):
+        if SCRATCH[out[1][0][0]][2] == I32:
+            op("G", lambda e: e.iota(out[0], pat, base, cm), [], [out])
+        else:
+            op("G", lambda e: e.iota(out[0], pat, base, cm, allow_small_or_imprecise_dtypes=True), [], [out])
+
+    def bc(x):
+        return ind(x, v("bcA"))
+
+    def wide(dst, x):
+        act(v(dst), bc(v(x)))
+
+    def last(name, a0=0, a1=16):
+        return v(name, a0 * 16 + 15, a1 * 16, 16)
+
+    half = W // 2
+    dma("Y", T.IV[:], T.vl[:], [], [v("IV")])
+    dma("S", T.IC[:], T.cl[:], [], [v("IC")])
+    dma("Y", T.X[:, 0:half], T.xc[:, 0:half], [], [v("X", 0, half)])
+    dma("S", T.X[:, half:W], T.xc[:, half:W], [], [v("X", half, W)])
+    dma("Y", T.LNI[0:8, :], T.ln[:], [], [v("LNI")])
+    dma("S", T.WI[:], T.wt[:], [], [v("WI")])
+    dma("Y", T.THI[0:8, :], T.th[:], [], [v("THI")])
+
+    iota(v("pcI"), [[0, 1]], 0, 1)
+    iota(v("MP"), [[0, 8], [1, 2], [0, 16]], 0, 0)
+    iota(v("iw", 0, 16), [[1, 16]], 0, 0)
+    iota(v("iw", 16, 32), [[16, 16]], 15, 0)
+    iota(v("QC"), [[0, 16], [1, 16]], 0, 0)
+    iota(v("mg"), [[1, 8], [0, 16]], 0, 0)
+    iota(v("mq"), [[0, 8], [1, 16]], 0, 0)
+    iota(v("mm"), [[1, 128]], 0, 0)
+    iota(v("cc"), [[1, 64]], 0, 0)
+    iota(v("bcI"), [[16, 4], [0, 16]], 0, 0)
+    iota(v("f2", 0, 16), [[16, 16]], W, 0)
+    ts(v("pmI"), v("pcI"), 15, OP.bitwise_and)
+    ts(v("p4I"), v("pcI"), 4, OP.arith_shift_right)
+    ts(v("btI"), v("p4I"), 1, OP.bitwise_and)
+    for a, b in (("pcF", "pcI"), ("pmF", "pmI"), ("p4F", "p4I"), ("btF", "btI")):
+        cp(v(a), v(b))
+    ts(v("MP"), v("MP"), v("btF"), OP.is_equal)
+    cp(v("bcA"), v("iw", 0, 16))
+    cp(v("bc15"), v("iw", 16, 32))
+
+    def conv(src, dst):
+        tr(v("CT1"), v(src))
+        cp(v("CIN2", 0, 240), v(src, 16, 256))
+        cp(v("CIN2", 240, 256), v(src, 0, 16))
+        tr(v("CT2"), v("CIN2"))
+        cp(v("CT3", 16, 256), v("CT2", 0, 240))
+        cp(v("CT3", 0, 16), v("CT2", 240, 256))
+        tt(v("m8"), v("CT1"), v("CT3"), OP.subtract)
+        tt(v("m9"), v("m8"), v("MP"), OP.mult)
+        tt(v(dst), v("m9"), v("CT3"), OP.add)
+
+    ts(v("m1"), v("IV"), 4096.0, OP.mult)
+    tt(v("VCA"), v("m1"), v("IC"), OP.add)
+    conv("VCA", "VCB")
+    cp(v("iw"), v("VCB"))
+    ts(v("IV"), v("iw"), 12, OP.arith_shift_right)
+    cp(v("LST", 0, 256), v("IV"))
+    ts(v("IC"), v("iw"), 4095, OP.bitwise_and)
+    cp(v("LST", 256, 511), v("IV", 1, 256))
+    cp(v("LST", 511, 512), v("IV", 255, 256))
+    cp(v("LST", 512, 768), v("IC"))
+
+    def consts1():
+        cp(v("V"), v("IV"))
+        cp(v("C"), v("IC"))
+        cp(v("N", 0, 255), v("V", 1, 256))
+        cp(v("N", 255, 256), v("V", 255, 256))
+        cp(v("V0"), v("V", 0, 256, 16))
+        ts(v("DG"), v("QC"), v("pmF"), OP.is_equal)
+        ts(v("RS"), v("QC"), 0.0, OP.is_gt)
+        op("V", lambda e: e.tensor_scalar(T.G8[0:8, :], T.mg[0:8, :], v("pcF", p=8)[0], None, OP.is_equal), [v("mg"), v("pcF")], [v("G8")])
+        op("V", lambda e: e.tensor_copy(T.LNF[0:8, :], T.LNI[0:8, :]), [v("LNI")], [v("LNF")])
+        op("V", lambda e: e.tensor_copy(T.THF[0:8, 0:1], T.THI[0:8, :]), [v("THI")], [v("THF")])
+        op("T", lambda e: e.matmul(T.pb0[:, 0:256], T.G8[0:8, :], T.LNF[0:8, :], True, True), [v("G8"), v("LNF")], [v("pb0", 0, 256)])
+        op("T", lambda e: e.matmul(T.pb1[:, 0:1], T.G8[0:8, :], T.THF[0:8, 0:1], True, True), [v("G8"), v("THF")], [v("pb1", 0, 1)])
+        cp(v("pb7", 0, 256), v("QC"))
+        cp(v("Pb"), v("QC"))
+        tt(v("f1"), v("pb0", 0, 256), v("DG"), OP.mult)
+        scan(v("f2"), v("RS"), v("f1"), OP.mult, OP.add)
+        cp(v("nn"), last("f2"))
+        ts(v("thm"), v("pb1", 0, 1), -8192.0, OP.add)
+        cp(v("lim"), v("thm"))
+        limits()
+        ts(v("Ident"), v("mm"), v("pcF"), OP.is_equal)
+        for nm, c in (("In1", -1.0), ("In2", -2.0), ("Ibig", BIG), ("Im256", -256.0), ("Im4k", -4096.0)):
+            ts(v(nm), v("Ident"), c, OP.mult)
+        fill(v("ones"), 1.0)
+
+    def consts2():
+        ts(v("blkF"), v("mg"), v("p4F"), OP.is_equal)
+        tt(v("f1", 0, 128), v("mq"), v("blkF"), OP.mult)
+        ts(v("f1", 128, 256), v("blkF"), -99.0, OP.mult, 99.0, OP.add)
+        tt(v("mq"), v("f1", 0, 128), v("f1", 128, 256), OP.add)
+        ts(v("e1"), v("pcF"), 0.0, OP.is_equal)
+        ts(v("e2"), v("pcF"), 1.0, OP.is_equal, 3840.0, OP.mult)
+        ts(v("ws"), v("pcF"), 2.0, OP.is_equal, -BIG, OP.mult)
+        tt(v("e2"), v("e2"), v("ws"), OP.add)
+        ts(v("CR"), v("cc"), v("e1"), OP.mult, v("e2"), OP.add)
+        for q in range(16):
+            ts(v("LQk", q * 128, q * 128 + 128), v("mq"), float(q), OP.is_equal, 4096.0, OP.mult)
+        ts(v("bcY"), v("bcI"), v("pmF"), OP.add)
+
+    def consts3():
+        for q in range(16):
+            ts(v("LQ1", q * 128, q * 128 + 128), v("mq"), float(q), OP.is_equal)
+
+    def consts4():
+        ts(v("wF"), v("WI"), -1.0, OP.mult)
+        for q in range(16):
+            ts(v("LW", q * 128, q * 128 + 128), v("mq"), float(q), OP.is_equal, v("wF"), OP.mult)
+        ts(v("LM"), v("QC"), v("pmF"), OP.is_gt)
+        ts(v("blk"), v("mg"), v("p4F"), OP.is_equal)
+        ts(v("blk8k"), v("blk"), 8192.0, OP.mult)
+        fill(v("onesF"), 1.0)
+        ts(v("G8T"), v("mm", 0, 8), v("p4F"), OP.is_equal)
+
+    ts(v("TR"), v("f2", 0, 16), v("pmF"), OP.add)
+
+    def limits():
+        ts(v("live"), v("nn"), 4.0, OP.is_ge)
+        ts(v("s8"), v("nn"), -2.0, OP.add)
+        ts(v("nl"), v("nn"), -1.0, OP.add)
+        tt(v("s9"), v("s8"), v("live"), OP.mult)
+        ts(v("ng"), v("s9"), -1.0, OP.add)
+        wide("ngB", "ng")
+        wide("nlB", "nl")
+
+    PP = v("pb7", 0, 256)
+
+    def masks():
+        tt(v("Vg"), v("ngB"), PP, OP.is_ge)
+        tt(v("VL"), v("nlB"), PP, OP.is_ge)
+        ts(v("m1"), v("Pb"), -4096.0, OP.mult, 65536.0, OP.add)
+        tt(v("PW"), v("m1"), v("V"), OP.add)
+
+    def dedupe(z, gap1, gap2):
+        tt(v("Hx"), bc(v(z)), v("DG"), OP.mult)
+        wide("zb", z)
+        mm(v("pb4", 0, 256), v("blkF"), v("Hx"), True, True)
+        gap1()
+        tt(v("pb0", 0, 256), v("pb4", 0, 256), v("LM"), OP.mult)
+        cp(v("Ru"), v("pb4", 0, 256))
+        tt(v("EQ", 0, 256), v("zb"), v("pb0", 0, 256), OP.is_equal)
+        mm(v("pb5", 0, 256), v("blk8k"), v("EQ", 0, 256), True, False)
+        at = 256
+        for a in range(15):
+            w = 240 - 16 * a
+            ts(v("EQ", at, at + w), v("Ru", 256 - w, 256), v(z, a, a + 1), OP.is_equal)
+            mm(v("pb5", 256 - w, 256), v("blk8k"), v("EQ", at, at + w), False, a == 14)
+            at += w
+        gap2()
+        tt(v("f1"), v("pb5", 0, 256), v("DG"), OP.mult)
+        scan(v("f2"), v("RS"), v("f1"), OP.mult, OP.add)
+        tt(v("s5"), last("f2"), v("hp"), OP.add)
+        tt(v("s5"), v("s5"), v("TR"), OP.min)
+        cp(v("off16"), v("s5"))
+
+    def send(buf, dst_buf, dst_rank, lsem, asem):
+        dst = T.cores[dst_rank]
+        rid, pid, _se = topo.addr(dst)
+        src = v(buf)
+        wait("G", need("G", src[1], []))
+        n = len(topo.engines(core, dst))
+        g.remote_dma(T[dst_buf][:], T[buf][:], T.sem[asem], T.sem[lsem], pid, rid, topo.mask(core, dst))
+        record("Gr", bump("G", lsem, n), src[1], [])
+
+    def arrive(buf, asem, src_rank):
+        n = len(topo.engines(T.cores[src_rank], core))
+        count[asem] = n
+        clock[(asem, n)] = {}
+        recs[buf] = [(0, 99999, (asem, n), "far", True)]
+
+    def gv(c):
+        act(v("GV%d" % c), ind(v("X", 0, W), v("LST", 64 * c, 64 * c + 64)))
+
+    gv(0)
+    consts1()
+    consts2()
+    for t in range(ST):
+        d = 1 + t % 3
+        to, frm = (rank + d) % 4, (rank - d) % 4
+        rL, rP, rY, rB = "rL%d" % t, "rP%d" % t, "rY%d" % t, "rB%d" % t
+        lastt = t == ST - 1
+
+        def gc(c):
+            act(v("GC%d" % c), ind(v("X", 0, W), v("LST", 512 + 64 * c, 512 + 64 * c + 64)))
+
+        def ss(c):
+            tt(v("SS%d" % c), ind(v("X", 0, W), v("LST", 256 + 64 * c, 256 + 64 * c + 64)), v("GV%d" % c), OP.add)
+
+        def dd(c):
+            for k in range(2):
+                b = "pb%d" % (2 * (c % 2) + k)
+                mm(v(b), v("Ident"), v("SS%d" % c, 512 * k, 512 * k + 512), True, False)
+                mm(v(b), v("In2"), v("GC%d" % c, 512 * k, 512 * k + 512), False, True)
+
+        def ab(c):
+            for k in range(2):
+                act(v("AB%d" % (c % 2), 512 * k, 512 * k + 512), v("pb%d" % (2 * (c % 2) + k)), AF.Abs)
+
+        def key(c):
+            o = v("pb%d" % (4 + c % 2), 0, 64)
+            mm(o, v("ones"), v("CR"), True, False)
+            mm(o, v("Im256"), v("Pb", 64 * c, 64 * c + 64), False, False)
+            mm(o, v("Ibig"), v("Vg", 64 * c, 64 * c + 64), False, False)
+            for q in range(16):
+                mm(o, v("LQk", 128 * q, 128 * q + 128), v("AB%d" % (c % 2), q, 1024, 16), False, q == 15)
+
+        def pick_a(c):
+            k = v("pb%d" % (4 + c % 2), 0, 64)
+            lo, hi = 64 * c, 64 * c + 64
+            a, b = 4 * c, 4 * c + 4
+            scan(v("SK", lo, hi), v("RS", 0, 64), k, OP.mult, OP.max)
+            ts(v("KA", a, b), last("SK", a, b), 63, OP.bitwise_and)
+            ts(v("o16", a, b), v("KA", a, b), 16.0, OP.mult, v("pmF"), OP.add)
+            cp(v("SYs", lo, hi), ind(v("SS%d" % c), v("o16", a, b)))
+            cp(v("KS", lo, hi), k)
+            tt(v("GYs", lo, hi), ind(v("GC%d" % c), v("o16", a, b)), v("SYs", lo, hi), OP.subtract)
+            ts(v("KB", a, b), last("SK", a, b), 3840, OP.bitwise_and)
+            ts(v("kp2", a, b), v("KB", a, b), -1.0 / 256, OP.mult, 17.0, OP.add)
+            ts(v("Yn", lo, hi), v("GYs", lo, hi), 0.0, OP.min, -63.0, OP.max)
+
+        def ee(c):
+            lo, hi = 64 * c, 64 * c + 64
+            tt(v("EE%d" % (c % 2)), ind(v("Yn", lo, hi), v("bcY")), v("GV%d" % c), OP.add)
+            tt(v("B3", lo, hi), ind(v("kp2"), v("bcA", 4 * c, 4 * c + 4)), v("Pb", lo, hi), OP.is_le)
+
+        def ae(c):
+            act(v("AE%d" % (c % 2)), v("EE%d" % (c % 2)), AF.Abs)
+
+        def ds(c):
+            lo, hi = 64 * c, 64 * c + 64
+            o = v("pb7", lo, hi)
+            mm(o, v("Im4k"), v("VL", lo, hi), True, False)
+            mm(o, v("Im4k"), v("B3", lo, hi), False, False)
+            for q in range(16):
+                mm(o, v("LQ1", 128 * q, 128 * q + 128), v("AE%d" % (c % 2), q, 1024, 16), False, q == 15)
+
+        send("LST", rL, to, "lR", "aR%d" % t)
+        for w in MEASURE.split():
+            if t == 0 and w == "ss2":
+                consts3()
+            if t == 0 and w == "ee2":
+                consts4()
+            if w == "masks":
+                masks()
+                send("Pb", rP, to, "lP", "aP%d" % t)
+            else:
+                {"ss": ss, "gc": gc, "gv": gv, "dd": dd, "ab": ab, "ky": key, "pk": pick_a, "ee": ee, "ae": ae, "ds": ds}[w[:2]](int(w[2:]))
+        act(v("kb"), ind(v("SK"), v("bc15")))
+        ee(3)
+        ae(3)
+        send("Yn", rY, to, "lY", "aY%d" % t)
+        for q in range(16):
+            mm(v("pb6", 0, 16), v("LW", 128 * q, 128 * q + 128), v("Yn", q, 256, 16), q == 0, q == 15)
+        ds(3)
+        OH, O15, KV, K2 = v("pb0", 256, 512), v("pb1", 0, 256), v("pb1", 256, 512), v("pb2", 0, 256)
+        t1, t2 = v("pb3", 0, 256), v("pb3", 256, 512)
+        act(v("pb2", 256, 512), v("Pb"))
+        act(v("Y"), v("Yn"), scale=-1.0)
+        tt(OH, v("kb"), v("KS"), OP.is_equal)
+        tt(v("m2"), v("V"), OH, OP.mult)
+        tt(v("m3"), v("N"), OH, OP.mult)
+        scan(v("m4"), v("RS"), v("m2"), OP.mult, OP.add)
+        scan(v("m5"), v("RS"), v("m3"), OP.mult, OP.add)
+        ts(v("K37"), last("m4"), 37.0, OP.mult)
+        cp(v("UI"), v("pb6", 0, 16))
+        cp(v("VK"), last("m4"))
+        ts(v("UI"), v("UI"), 4095, OP.bitwise_and)
+        cp(v("NK"), last("m5"))
+        tt(v("HI"), v("UI"), v("UI"), OP.mult)
+        ts(v("kq"), v("kp2"), -1.0, OP.mult, 17.0, OP.add)
+        ts(v("HI"), v("HI"), 5, OP.arith_shift_right)
+        cp(v("SB", 32, 48), last("m5"))
+        tt(v("HI"), v("HI"), v("K37"), OP.add)
+        ts(v("SB", 16, 32), v("kp2"), -1.0, OP.mult, 17.0, OP.add)
+        ts(v("HI"), v("HI"), 4095, OP.bitwise_and)
+        wide("NKB", "NK")
+        wide("VKB", "VK")
+        ts(v("rest"), v("kq"), 0.0, OP.is_equal)
+        ts(v("hm"), v("HI"), 16384.0, OP.subtract)
+        ts(v("s4"), v("HI"), 2.0, OP.add)
+        F = v("pb0", 0, 256)
+        ts(F, v("pb7", 0, 256), v("lim"), OP.is_le)
+        tt(v("m1"), F, v("PW"), OP.mult)
+        scan(v("SM"), v("RS"), v("m1"), OP.mult, OP.max)
+        ts(v("MX"), last("SM"), 12, OP.arith_shift_right)
+        ts(v("VM"), last("SM"), 4095, OP.bitwise_and)
+        ts(v("close"), v("MX"), 0.0, OP.is_gt)
+        tt(v("s1"), v("kq"), v("MX"), OP.subtract)
+        ts(v("s2"), v("MX"), 0.0, OP.is_equal)
+        tt(v("SB", 0, 16), v("s1"), v("close"), OP.mult)
+        send("SB", rB, to, "lB", "aB%d" % t)
+        tt(v("grow"), v("s2"), v("live"), OP.mult)
+        tt(v("s4"), v("s4"), v("grow"), OP.mult)
+        ts(v("zL"), v("s4"), -1.0, OP.add)
+        tt(v("s7"), v("HI"), v("grow"), OP.mult)
+        ts(v("s6"), v("grow"), 16.0, OP.mult, -1.0, OP.add)
+        wide("s6B", "s6")
+        tt(v("x"), v("s7"), v("VM"), OP.add)
+
+        def gap1():
+            wide("xB", "x")
+            tt(v("s8"), v("hm"), v("grow"), OP.mult)
+            tt(v("s3"), v("nn"), v("grow"), OP.add)
+            ts(v("hp"), v("s8"), 16384.0, OP.add)
+            ts(v("s3"), v("s3"), 16.0, OP.min)
+            tt(O15, v("s6B"), v("pb2", 256, 512), OP.is_equal)
+            tt(v("nn"), v("s3"), v("SB", 0, 16), OP.subtract)
+            act(KV, O15, AF.Identity, scale=-1.0, bias=1.0)
+            act(v("KVs"), O15, AF.Identity, scale=-1.0, bias=1.0)
+            op("V", lambda e: e.tensor_reduce(v("cs1")[0], v("close")[0], AxisListType.X, OP.add), [v("close")], [v("cs1")])
+            tt(v("MXe"), v("MX"), v("grow"), OP.add)
+
+        def gap2():
+            mm(v("pb6", 0, 1), v("onesF"), v("cs1"), True, True)
+            tt(K2, v("KVs"), OH, OP.subtract)
+            tt(v("m7"), v("xB"), O15, OP.mult)
+            tt(t1, v("V"), KV, OP.mult)
+            tt(v("V"), t1, v("m7"), OP.add)
+
+        dedupe("zL", gap1, gap2)
+        cp(ind(v("X"), v("off16")), v("Y"))
+        if not lastt:
+            tt(v("m8"), v("xB"), OH, OP.mult)
+            tt(v("m9"), v("NKB"), O15, OP.mult)
+            tt(t1, v("N"), K2, OP.mult)
+            tt(t2, t1, v("m8"), OP.add)
+            tt(v("N"), t2, v("m9"), OP.add)
+        tt(v("m6"), v("VKB"), O15, OP.mult)
+        tt(t1, v("C"), K2, OP.mult)
+        tt(t2, t1, v("m3"), OP.add)
+        tt(v("C"), t2, v("m6"), OP.add)
+        cp(v("cI"), v("pb6", 0, 1))
+        ts(v("cI"), v("cI"), 31, OP.bitwise_and)
+        tt(v("lim"), v("thm"), v("cI"), OP.add)
+        for m, b in (("R", rL), ("P", rP), ("Y", rY), ("B", rB)):
+            arrive(b, "a%s%d" % (m, t), frm)
+        e_, k_, n_ = v(rB, 0, 16), v(rB, 16, 32), v(rB, 32, 48)
+        tt(v("s1"), e_, v("nn"), OP.is_gt)
+        tt(v("s2"), n_, v("V0"), OP.subtract)
+        tt(v("take"), v("s1"), v("rest"), OP.mult)
+        tt(v("s3"), e_, v("nn"), OP.subtract)
+        wide("TKb", "take")
+        act(v("pb1", 0, 256), v("TKb"))
+        act(v("pb1", 256, 512), v("TKb"), AF.Identity, scale=-1.0, bias=1.0)
+        TP, NT = v("pb1", 0, 256), v("pb1", 256, 512)
+        tt(v("s2"), v("s2"), v("take"), OP.mult)
+        tt(v("s3"), v("s3"), v("take"), OP.mult)
+        tt(v("V0"), v("V0"), v("s2"), OP.add)
+        tt(v("nn"), v("nn"), v("s3"), OP.add)
+        ts(v("s4"), k_, 0.0, OP.is_gt)
+        ts(v("s6"), v("nn"), 1.0, OP.is_ge)
+        ts(v("s5"), v("V0"), 2.0, OP.add)
+        tt(v("s6"), v("s6"), v("s4"), OP.mult)
+        ts(v("hm"), v("V0"), 16384.0, OP.subtract)
+        tt(v("s5"), v("s5"), v("s6"), OP.mult)
+        cp(v("z16"), v("V0"))
+        ts(v("zL"), v("s5"), -1.0, OP.add)
+
+        def take(own, k):
+            cp(t1, v(rL, 256 * k, 256 * k + 256))
+            tt(v("m2"), v(own), NT, OP.mult)
+            tt(t2, t1, v("TKb"), OP.mult)
+            tt(v(own), t2, v("m2"), OP.add)
+            if not lastt:
+                cp(v("LST", 256 * k, 256 * k + 256), v(own))
+
+        def gap3():
+            tt(v("s7"), v("take"), k_, OP.mult)
+            ts(v("s8"), v("take"), 16.0, OP.mult)
+            tt(v("MXe"), v("MXe"), v("s7"), OP.add)
+            tt(v("kqe"), v("kq"), v("s8"), OP.add)
+            wide("MXB", "MXe")
+            wide("kqB", "kqe")
+            act(v("kthB"), v("kqB"), AF.Identity, scale=-1.0, bias=15.0)
+            act(v("mthB"), v("MXB"), AF.Identity, scale=-1.0, bias=16.0)
+            take("V", 0)
+            limits()
+            tt(v("s7"), v("hm"), v("s6"), OP.mult)
+            ts(v("hp"), v("s7"), 16384.0, OP.add)
+
+        def gap4():
+            tt(v("Pa"), v("Pb"), NT, OP.mult)
+            tt(v("Pr"), v(rP), TP, OP.mult)
+            PS = v("pb6", 0, 256)
+            mm(PS, v("Ident"), v("Pa"), True, False)
+            mm(PS, v("Ident"), v("Pr"), False, True)
+            tt(v("BL"), ind(v("X", 0, W), v("z16")), v(rY), OP.subtract)
+            ts(v("BL2"), v("BL"), 0.5, OP.mult, 159.75, OP.add)
+            ts(v("BL"), v("BL2"), -160.0, OP.add)
+            if not lastt:
+                take("N", 1)
+
+        dedupe("zL", gap3, gap4)
+        cp(ind(v("X"), v("off16")), v("BL"))
+        if lastt:
+            dma("Y", T.yx[:, 0:half], T.X[:, 0:half], [v("X", 0, half)], [])
+            dma("S", T.yx[:, half:W], T.X[:, half:W], [v("X", half, W)], [])
+        else:
+            gv(0)
+        take("C", 2)
+        PS, ga, gb = v("pb6", 0, 256), v("pb2", 0, 256), v("pb2", 256, 512)
+        tt(ga, v("kthB"), PS, OP.is_lt)
+        tt(gb, v("mthB"), PS, OP.is_le)
+        tt(v("g1"), v("MXB"), ga, OP.mult)
+        tt(v("g2"), v("kqB"), gb, OP.mult)
+        mm(PP, v("Ident"), v("Pa"), True, False)
+        mm(PP, v("Ident"), v("Pr"), False, False)
+        mm(PP, v("Ident"), v("g1"), False, False)
+        mm(PP, v("In1"), v("g2"), False, True)
+        cp(v("Pb"), PP)
+
+    tt(v("Hx"), bc(v("nn")), v("DG"), OP.mult)
+    op("T", lambda e: e.matmul(T.pb4[0:8, 0:256], T.G8T[:], v("Hx")[0], True, True), [v("G8T"), v("Hx")], [v("pb4", 0, 256)])
+    ts(v("m7"), v("V"), 4096.0, OP.mult)
+    tt(v("VCA"), v("m7"), v("C"), OP.add)
+    tt(v("pb3", 0, 256), v("nlB"), PP, OP.is_ge)
+    ts(v("m6"), v("pb3", 0, 256), -100.0, OP.mult, 100.0, OP.add)
+    tt(v("m1"), PP, v("m6"), OP.add)
+    op("V", lambda e: e.tensor_copy(T.LNF[0:8, :], T.pb4[0:8, 0:256]), [v("pb4", 0, 256)], [v("LNF")])
+    dma("Y", T.yn[:], T.LNF[0:8, :], [v("LNF")], [])
+    for p in range(0, 16, 2):
+        bs = v("pb%d" % (2 + p // 2 % 2), 0, 256)
+        ts(v("pb%d" % (p // 2 % 2), 0, 256), v("m1"), float(p), OP.is_equal)
+        for j in range(2):
+            b = v("pb%d" % (p // 2 % 2), 0, 256)
+            if j == 1:
+                ts(b, v("m1"), float(p + 1), OP.is_equal)
+            pr, sn = v("m%d" % (2 + (p + j) % 3)), "m%d" % (5 + (p + j) % 3) if (p + j) % 3 != 1 else "f2"
+            tt(pr, b, v("VCA"), OP.mult)
+            scan(v(sn), v("RS"), pr, OP.mult, OP.add)
+            act(v("SO", p + j, 256, 16), last(sn))
+    conv("SO", "VCB")
+    cp(v("iw"), v("VCB"))
+    ts(v("IV"), v("iw"), 12, OP.arith_shift_right)
+    ts(v("IC"), v("iw"), 4095, OP.bitwise_and)
+    cp(v("V"), v("IV"))
+    dma("Y", T.yv[:], T.V[:], [v("V")], [])
+    cp(v("C"), v("IC"))
+    dma("S", T.yc[:], T.C[:], [v("C")], [])
+    for s in sorted(count):
+        if known["G"].get(s, 0) < count[s]:
+            g.wait_ge(T.sem[s], count[s])

@@ -6,8 +6,10 @@ W, L, S, ST = 4096, 256, 16, 5
 BIG = 8388608.0
 F32, BF, I32, U16 = "float32", "bfloat16", "int32", "uint16"
 
-MEASURE = ("gc0 ss0 masks gv1 ss1 dd0 ab0 ky0 pk0 gc1 dd1 gv2 ee0 ab1 ss2 ky1 ae0 gc2 dd2 gv3 ab2 ds0 gc3 "
-           "pk1 ky2 ee1 ss3 pk2 ee2 ae1 dd3 ab3 ae2 ky3 ds1 ds2 pk3")
+MEASURE = ("gc0 ss0 gv1 ss1 dd0 ab0 ky0 pk0 gc1 dd1 gv2 ee0 ab1 ss2 ky1 gc2 dd2 gv3 ab2 ds0 gc3 "
+           "pk1 ky2 ee1 ss3 pk2 ds1 ee2 dd3 ab3 ky3 ds2 pk3 ee3 ds3")
+CYC, GATHER, SCATTER, WAKE, SLACK = 0.001, 1.5, 3.8, 0.08, 0.02
+BETA = 0.1
 SCRATCH = {"X": ("sbuf", [128, W + L], BF)}
 ALIAS = {}
 
@@ -26,31 +28,34 @@ def _add(names, cols, d):
 
 for _c in range(4):
     _add("GV%d SS%d GC%d" % (_c, _c, _c), 1024, BF)
-_add("AB0 AB1 EE0 EE1 AE0 AE1", 1024, BF)
-_add("V N C VCB CIN2 CT1 CT2 DG", 256, F32)
-_pack("MF", "PW m1 m2 m3 m4 m5 m6 m7 m8 m9 KS LM RS MP CT3 QC Hx f1 f2 SO VCA kb s6B zb xB NKB VKB TKb kthB mthB MXB kqB ngB nlB KVs", 256, F32)
+_add("AB0 AB1 EE0 EE1", 1024, BF)
+_pack("VNC", "V N C", 256, F32)
+_add("VCB CIN2 CT1 CT2 DG", 256, F32)
+_pack("MF", "PW m1 m2 m3 m4 m5 m6 m7 m8 m9 KS LM RS MP CT3 QC Hx f1 f2 SO VCA kb s6B zb xB NKB VKB TKb kthB mthB MXB kqB ngB nlB KVs TB nC oC "
+      "m1' m2' m3' m4' m5' m6' m7' m8' m9' Hx' f1' f2' zb'", 256, F32)
 _add("SK SM IV IC iw LNI", 256, I32)
 _add("Pb Vg VL B3 Y Yn SYs GYs BL BL2 Pa Pr g1 g2", 256, BF)
 _add("LST", 768, U16)
-_add("Ru", 256, U16)
-_add("EQ", 2176, BF)
-_pack("PLF", "nn V0 live kq kp2 VK NK ng nl close grow gsel rest MXe TR hm hp cnt s1 s2 s3 s4 s5 s6 s7 s8 s9 zL take kqe mth kth x", 16, F32)
+_pack("RR", "Ru Ru'", 256, U16)
+_pack("EQQ", "EQ EQ'", 2176, BF)
+_pack("PLF", "nn V0 live kq kp2 VK NK ng nl close grow gsel rest MXe TR hm hp cnt s1 s2 s3 s4 s5 s6 s7 s8 s9 zL take kqe mth kth x Tl "
+      "s1' s2' s3' s4' s5' s6' s7' s8' s9' hp' zL' has", 16, F32)
 _pack("PLI", "KA KB UI HI K37 MX VM", 16, I32)
 _pack("PLU", "o16 off16 z16 bcA bc15", 16, U16)
 _add("bcY", 64, U16)
 _pack("COF", "pcF pmF p4F btF thm lim cs1 e1 e2 wF ws", 1, F32)
 _pack("COI", "pcI pmI p4I btI cI", 1, I32)
 _add("WI THI", 1, I32)
-_add("mq mg mm blkF onesF G8", 128, F32)
+_add("mq mg mm blkF onesF G8 IdF", 128, F32)
 _pack("IDS", "Ident In1 In2 Ibig Im256 Im4k ones blk blk8k", 128, BF)
-_add("LQ1 LQk LW", 2048, BF)
+_add("LQ1 LQk LQh LW", 2048, BF)
 _add("CR", 64, BF)
 _add("cc", 64, F32)
 _add("LNF THF", 256, F32)
 _add("G8T", 8, F32)
 _add("bcI", 64, I32)
 for _t in range(ST):
-    _add("rL%d" % _t, 768, U16)
+    _add("rL%d" % _t, 768, F32)
     _add("rP%d rY%d" % (_t, _t), 256, BF)
     _add("rB%d" % _t, 48, F32)
 _add("SB", 48, F32)
@@ -73,7 +78,11 @@ def rank_program(g, core, T, topo):
     recs = {}
     ndma = [0]
 
+    par = [0]
+
     def v(name, lo=0, hi=None, step=1, p=None):
+        if par[0] and name + "'" in ALIAS:
+            name += "'"
         if name in ALIAS:
             name, at, width, _d = ALIAS[name]
             hi = at + (width if hi is None else hi)
@@ -81,10 +90,10 @@ def rank_program(g, core, T, topo):
         hi = SCRATCH[name][1][1] if hi is None else hi
         t = T[name]
         sl = slice(lo, hi, step) if step != 1 else slice(lo, hi)
-        return (t[:, sl] if p is None else t[0:p, sl], [(name, lo, hi)])
+        return (t[:, sl] if p is None else t[0:p, sl], [(name, lo, hi)], (hi - lo + step - 1) // step, False)
 
     def ind(win, off):
-        return (win[0].indirect(off[0]), win[1] + off[1])
+        return (win[0].indirect(off[0]), win[1] + off[1], off[2] * 16, True)
 
     def need(q, reads, writes):
         toks = []
@@ -135,65 +144,156 @@ def rank_program(g, core, T, topo):
         clock[tok] = dict(known[q])
         return tok
 
-    def op(q, fn, reads, writes):
-        rd = [a for x in reads for a in x[1]]
-        wr = [a for x in writes for a in x[1]]
-        wait(q, need(q, rd, wr))
-        inst = fn(queues[q])
-        sem = "s" + q
-        inst.then_inc(T.sem[sem], 1)
-        record(q, bump(q, sem, 1), rd, wr)
+    OPS = []
+
+    def add(q, emit, reads, writes, cost, lat=0.0, after=()):
+        OPS.append([q, emit, [a for x in reads for a in x[1]], [a for x in writes for a in x[1]], cost, lat, list(after)])
+        return len(OPS) - 1
+
+    def op(q, fn, reads, writes, cost=0.06):
+        def emit(rd, wr):
+            wait(q, need(q, rd, wr))
+            sem = "s" + q
+            fn(queues[q]).then_inc(T.sem[sem], 1)
+            record(q, bump(q, sem, 1), rd, wr)
+        return add(q, emit, reads, writes, cost)
 
     def dma(q, out, in_, reads=(), writes=()):
-        rd = [a for x in reads for a in x[1]]
-        wr = [a for x in writes for a in x[1]]
-        wait(q, need(q, rd, wr))
         sem = "d%d" % ndma[0]
         ndma[0] += 1
-        queues[q].dma_start(out, in_).then_inc(T.sem[sem], 16)
-        record(q + "d", bump(q, sem, 16), rd, wr)
+
+        def emit(rd, wr):
+            wait(q, need(q, rd, wr))
+            queues[q].dma_start(out, in_).then_inc(T.sem[sem], 16)
+            record(q + "d", bump(q, sem, 16), rd, wr)
+        return add(q, emit, reads, writes, 0.1, 5.0 if writes and writes[0][1][0][0] == "X" else 2.2)
+
+    def order():
+        seen, deps, succ = {}, [], [[] for _ in OPS]
+        for i, o in enumerate(OPS):
+            q, dp = o[0], {}
+            for j in o[6]:
+                dp[j] = 1
+            for acc, wr in [(a, 0) for a in o[2]] + [(a, 1) for a in o[3]]:
+                name, lo, hi = acc
+                bank = name.startswith("pb")
+                if bank and seen.get(name) and seen[name][0][3] != q:
+                    seen[name, "before"] = seen.pop(name)
+                for r in seen.get((name, "before"), []):
+                    dp[r[2]] = 1
+                for (l2, h2, j, q2, w2) in seen.get(name, []):
+                    if bank and q == "T":
+                        dp[j] = max(dp.get(j, 0), 0)
+                    elif lo < h2 and l2 < hi and (wr or w2):
+                        dp[j] = 1
+            for acc, wr in [(a, 0) for a in o[2]] + [(a, 1) for a in o[3]]:
+                name, lo, hi = acc
+                old = seen.get(name, [])
+                if wr:
+                    old = [r for r in old if not (lo <= r[0] and r[1] <= hi)]
+                seen[name] = old + [(lo, hi, i, q, wr)]
+            dp.pop(i, None)
+            deps.append(dp)
+            for j in dp:
+                succ[j].append(i)
+        n = len(OPS)
+        prio = [0.0] * n
+        for i in range(n - 1, -1, -1):
+            prio[i] = OPS[i][4] + OPS[i][5] + max([prio[j] + (WAKE if deps[j][i] else -OPS[i][4]) for j in succ[i]] or [0.0])
+        left = [len(dp) for dp in deps]
+        start, fin = [0.0] * n, [0.0] * n
+        free, ready, out = {}, {}, []
+
+        def push(i):
+            r = 0.0
+            for j, k in deps[i].items():
+                r = max(r, fin[j] + WAKE if k else start[j])
+            ready.setdefault(OPS[i][0], []).append((r, BETA * i - prio[i], i))
+        for i in range(n):
+            if left[i] == 0:
+                push(i)
+        while len(out) < n:
+            best = None
+            for q, lst in ready.items():
+                if lst:
+                    t0 = max(free.get(q, 0.0), min(lst)[0])
+                    p, i, r = min((c[1], c[2], c) for c in lst if c[0] <= t0 + SLACK)
+                    st = max(t0, r[0])
+                    if best is None or st < best[0]:
+                        best = (st, q, i, r)
+            st, q, i, r = best
+            ready[q].remove(r)
+            start[i] = st
+            fin[i] = st + OPS[i][4] + OPS[i][5]
+            free[q] = st + OPS[i][4]
+            out.append(i)
+            for j in succ[i]:
+                left[j] -= 1
+                if left[j] == 0:
+                    push(j)
+        return out
+
+    def vcost(out, a, b=None):
+        views = [x for x in (out, a, b) if x is not None]
+        if out[3]:
+            return 0.06 + SCATTER * CYC * out[2]
+        if any(x[3] for x in views):
+            return 0.06 + GATHER * CYC * out[2]
+        n = max(out[2], a[2])
+        psum = any(x[1][0][0].startswith("pb") for x in views[1:])
+        small = all(SCRATCH[x[1][0][0]][2] in (BF, U16) for x in views)
+        if b is not None:
+            n *= 1 if psum else 2
+        elif small:
+            n *= 0.5
+        return max(64, n) * CYC
 
     def tt(out, a, b, o):
-        op("V", lambda e: e.tensor_tensor(out[0], a[0], b[0], o), [a, b], [out])
+        op("V", lambda e: e.tensor_tensor(out[0], a[0], b[0], o), [a, b], [out], vcost(out, a, b))
 
     def ts(out, a, s1, o0, s2=None, o1=None):
         rd = [a] + [x for x in (s1, s2) if isinstance(x, tuple)]
         x1 = s1[0] if isinstance(s1, tuple) else s1
         x2 = s2[0] if isinstance(s2, tuple) else s2
         if o1 is None:
-            op("V", lambda e: e.tensor_scalar(out[0], a[0], x1, None, o0), rd, [out])
+            op("V", lambda e: e.tensor_scalar(out[0], a[0], x1, None, o0), rd, [out], vcost(out, a))
         else:
-            op("V", lambda e: e.tensor_scalar(out[0], a[0], x1, x2, o0, o1), rd, [out])
+            op("V", lambda e: e.tensor_scalar(out[0], a[0], x1, x2, o0, o1), rd, [out], vcost(out, a))
 
     def cp(out, a):
-        op("V", lambda e: e.tensor_copy(out[0], a[0]), [a], [out])
+        op("V", lambda e: e.tensor_copy(out[0], a[0]), [a], [out], vcost(out, a))
 
     def act(out, a, f=AF.Copy, scale=1.0, bias=0.0):
-        op("S", lambda e: e.activation(out[0], a[0], f, bias=bias, scale=scale), [a], [out])
+        c = (0.07 + GATHER * CYC * out[2]) if a[3] else 0.06 + CYC * max(64, out[2])
+        op("S", lambda e: e.activation(out[0], a[0], f, bias=bias, scale=scale), [a], [out], c)
 
     def mm(out, l, r, start, stop):
-        op("T", lambda e: e.matmul(out[0], l[0], r[0], start, stop), [l, r], [out])
+        c = max(64, r[2]) * CYC * (4 if SCRATCH[r[1][0][0]][2] == F32 else 1)
+        op("T", lambda e: e.matmul(out[0], l[0], r[0], start, stop), [l, r], [out], c)
 
     def scan(out, d0, d1, o0, o1):
-        op("V", lambda e: e.tensor_tensor_scan(out[0], d0[0], d1[0], 0.0, o0, o1), [d0, d1], [out])
+        op("V", lambda e: e.tensor_tensor_scan(out[0], d0[0], d1[0], 0.0, o0, o1), [d0, d1], [out], max(64, out[2]) * CYC)
 
     def tr(out, a):
-        op("V", lambda e: e.transpose(out[0], a[0]), [a], [out])
+        op("V", lambda e: e.transpose(out[0], a[0]), [a], [out], vcost(out, a))
 
     def fill(out, c):
         op("V", lambda e: e.memset(out[0], c), [], [out])
 
     def iota(out, pat, base, cm):
         if SCRATCH[out[1][0][0]][2] == I32:
-            op("G", lambda e: e.iota(out[0], pat, base, cm), [], [out])
+            op("G", lambda e: e.iota(out[0], pat, base, cm), [], [out], 0.13 + 2 * CYC * out[2])
         else:
-            op("G", lambda e: e.iota(out[0], pat, base, cm, allow_small_or_imprecise_dtypes=True), [], [out])
+            op("G", lambda e: e.iota(out[0], pat, base, cm, allow_small_or_imprecise_dtypes=True), [], [out], 0.13 + 2 * CYC * out[2])
 
     def bc(x):
         return ind(x, v("bcA"))
 
-    def wide(dst, x):
-        act(v(dst), bc(v(x)))
+    def wide(dst, x, scale=1.0, bias=0.0):
+        act(v(dst), bc(v(x)), AF.Copy if (scale, bias) == (1.0, 0.0) else AF.Identity, scale, bias)
+
+    def line(dst, x, scale, bias):
+        act(dst, x, AF.Identity, scale, bias)
 
     def last(name, a0=0, a1=16):
         return v(name, a0 * 16 + 15, a1 * 16, 16)
@@ -217,7 +317,7 @@ def rank_program(g, core, T, topo):
     iota(v("mm"), [[1, 128]], 0, 0)
     iota(v("cc"), [[1, 64]], 0, 0)
     iota(v("bcI"), [[16, 4], [0, 16]], 0, 0)
-    iota(v("f2", 0, 16), [[16, 16]], W, 0)
+    iota(v("f2", 0, 16), [[16, 16]], W + 1, 0)
     ts(v("pmI"), v("pcI"), 15, OP.bitwise_and)
     ts(v("p4I"), v("pcI"), 4, OP.arith_shift_right)
     ts(v("btI"), v("p4I"), 1, OP.bitwise_and)
@@ -263,17 +363,17 @@ def rank_program(g, core, T, topo):
         op("T", lambda e: e.matmul(T.pb0[:, 0:256], T.G8[0:8, :], T.LNF[0:8, :], True, True), [v("G8"), v("LNF")], [v("pb0", 0, 256)])
         op("T", lambda e: e.matmul(T.pb1[:, 0:1], T.G8[0:8, :], T.THF[0:8, 0:1], True, True), [v("G8"), v("THF")], [v("pb1", 0, 1)])
         cp(v("pb7", 0, 256), v("QC"))
-        cp(v("Pb"), v("QC"))
         tt(v("f1"), v("pb0", 0, 256), v("DG"), OP.mult)
         scan(v("f2"), v("RS"), v("f1"), OP.mult, OP.add)
         cp(v("nn"), last("f2"))
-        ts(v("thm"), v("pb1", 0, 1), -8192.0, OP.add)
+        ts(v("thm"), v("pb1", 0, 1), 0.5, OP.mult, -8192.0, OP.add)
         cp(v("lim"), v("thm"))
         limits()
         ts(v("Ident"), v("mm"), v("pcF"), OP.is_equal)
         for nm, c in (("In1", -1.0), ("In2", -2.0), ("Ibig", BIG), ("Im256", -256.0), ("Im4k", -4096.0)):
             ts(v(nm), v("Ident"), c, OP.mult)
         fill(v("ones"), 1.0)
+        ts(v("IdF"), v("mm"), v("pcF"), OP.is_equal)
 
     def consts2():
         ts(v("blkF"), v("mg"), v("p4F"), OP.is_equal)
@@ -286,17 +386,12 @@ def rank_program(g, core, T, topo):
         tt(v("e2"), v("e2"), v("ws"), OP.add)
         ts(v("CR"), v("cc"), v("e1"), OP.mult, v("e2"), OP.add)
         for q in range(16):
-            ts(v("LQk", q * 128, q * 128 + 128), v("mq"), float(q), OP.is_equal, 4096.0, OP.mult)
-        ts(v("bcY"), v("bcI"), v("pmF"), OP.add)
-
-    def consts3():
-        for q in range(16):
             ts(v("LQ1", q * 128, q * 128 + 128), v("mq"), float(q), OP.is_equal)
-
-    def consts4():
-        ts(v("wF"), v("WI"), -1.0, OP.mult)
-        for q in range(16):
-            ts(v("LW", q * 128, q * 128 + 128), v("mq"), float(q), OP.is_equal, v("wF"), OP.mult)
+        ts(v("LQk"), v("LQ1"), 4096.0, OP.mult)
+        ts(v("bcY"), v("bcI"), v("pmF"), OP.add)
+        ts(v("LQh"), v("LQ1"), -0.5, OP.mult)
+        cp(v("wF"), v("WI"))
+        ts(v("LW"), v("LQ1"), v("wF"), OP.mult)
         ts(v("LM"), v("QC"), v("pmF"), OP.is_gt)
         ts(v("blk"), v("mg"), v("p4F"), OP.is_equal)
         ts(v("blk8k"), v("blk"), 8192.0, OP.mult)
@@ -307,19 +402,16 @@ def rank_program(g, core, T, topo):
 
     def limits():
         ts(v("live"), v("nn"), 4.0, OP.is_ge)
-        ts(v("s8"), v("nn"), -2.0, OP.add)
-        ts(v("nl"), v("nn"), -1.0, OP.add)
-        tt(v("s9"), v("s8"), v("live"), OP.mult)
-        ts(v("ng"), v("s9"), -1.0, OP.add)
-        wide("ngB", "ng")
-        wide("nlB", "nl")
+        wide("ngB", "nn", 1.08, -3.29)
+        wide("nlB", "nn", 1.0, -1.0)
 
     PP = v("pb7", 0, 256)
 
     def masks():
+        act(v("m1"), PP, AF.Identity, scale=-4096.0, bias=65536.0)
+        act(v("Pb"), PP)
         tt(v("Vg"), v("ngB"), PP, OP.is_ge)
         tt(v("VL"), v("nlB"), PP, OP.is_ge)
-        ts(v("m1"), v("Pb"), -4096.0, OP.mult, 65536.0, OP.add)
         tt(v("PW"), v("m1"), v("V"), OP.add)
 
     def dedupe(z, gap1, gap2):
@@ -341,23 +433,35 @@ def rank_program(g, core, T, topo):
         tt(v("f1"), v("pb5", 0, 256), v("DG"), OP.mult)
         scan(v("f2"), v("RS"), v("f1"), OP.mult, OP.add)
         tt(v("s5"), last("f2"), v("hp"), OP.add)
-        tt(v("s5"), v("s5"), v("TR"), OP.min)
-        cp(v("off16"), v("s5"))
+        tt(v("s8"), v("s5"), v("TR"), OP.min)
+        ts(v("off16"), v("s8"), -1.0, OP.add)
+
+    def names(z, yes):
+        tt(v("s7"), v(z), v(yes), OP.mult)
+        line(v("s9"), v(yes), 2.0, -1.0)
+        line(v("s6"), v(yes), -16384.0, 16384.0)
+        tt(v("zL"), v("s7"), v("s9"), OP.add)
+        tt(v("hp"), v("s6"), v("zL"), OP.add)
 
     def send(buf, dst_buf, dst_rank, lsem, asem):
         dst = T.cores[dst_rank]
         rid, pid, _se = topo.addr(dst)
-        src = v(buf)
-        wait("G", need("G", src[1], []))
         n = len(topo.engines(core, dst))
-        g.remote_dma(T[dst_buf][:], T[buf][:], T.sem[asem], T.sem[lsem], pid, rid, topo.mask(core, dst))
-        record("Gr", bump("G", lsem, n), src[1], [])
 
-    def arrive(buf, asem, src_rank):
+        def emit(rd, wr):
+            wait("G", need("G", rd, wr))
+            g.remote_dma(T[dst_buf][:], T[buf][:], T.sem[asem], T.sem[lsem], pid, rid, topo.mask(core, dst))
+            record("Gr", bump("G", lsem, n), rd, wr)
+        return add("G", emit, [v(buf)], [], 1.5, 3.0)
+
+    def arrive(buf, asem, src_rank, sent):
         n = len(topo.engines(T.cores[src_rank], core))
-        count[asem] = n
-        clock[(asem, n)] = {}
-        recs[buf] = [(0, 99999, (asem, n), "far", True)]
+
+        def emit(rd, wr):
+            count[asem] = n
+            clock[(asem, n)] = {}
+            recs[buf] = [(0, 99999, (asem, n), "far", True)]
+        add("F", emit, [], [v(buf)], 0.0, 1.0, [sent])
 
     def gv(c):
         act(v("GV%d" % c), ind(v("X", 0, W), v("LST", 64 * c, 64 * c + 64)))
@@ -402,97 +506,82 @@ def rank_program(g, core, T, topo):
             scan(v("SK", lo, hi), v("RS", 0, 64), k, OP.mult, OP.max)
             ts(v("KA", a, b), last("SK", a, b), 63, OP.bitwise_and)
             ts(v("o16", a, b), v("KA", a, b), 16.0, OP.mult, v("pmF"), OP.add)
-            cp(v("SYs", lo, hi), ind(v("SS%d" % c), v("o16", a, b)))
-            cp(v("KS", lo, hi), k)
-            tt(v("GYs", lo, hi), ind(v("GC%d" % c), v("o16", a, b)), v("SYs", lo, hi), OP.subtract)
+            cp(v("SYs", lo, hi), ind(v("GC%d" % c), v("o16", a, b)))
+            act(v("KS", lo, hi), k)
+            tt(v("GYs", lo, hi), ind(v("SS%d" % c), v("o16", a, b)), v("SYs", lo, hi), OP.subtract)
             ts(v("KB", a, b), last("SK", a, b), 3840, OP.bitwise_and)
             ts(v("kp2", a, b), v("KB", a, b), -1.0 / 256, OP.mult, 17.0, OP.add)
-            ts(v("Yn", lo, hi), v("GYs", lo, hi), 0.0, OP.min, -63.0, OP.max)
+            ts(v("Y", lo, hi), v("GYs", lo, hi), 0.0, OP.max, 63.0, OP.min)
 
         def ee(c):
             lo, hi = 64 * c, 64 * c + 64
-            tt(v("EE%d" % (c % 2)), ind(v("Yn", lo, hi), v("bcY")), v("GV%d" % c), OP.add)
+            tt(v("EE%d" % (c % 2)), ind(v("Y", lo, hi), v("bcY")), v("GV%d" % c), OP.max)
             tt(v("B3", lo, hi), ind(v("kp2"), v("bcA", 4 * c, 4 * c + 4)), v("Pb", lo, hi), OP.is_le)
-
-        def ae(c):
-            act(v("AE%d" % (c % 2)), v("EE%d" % (c % 2)), AF.Abs)
 
         def ds(c):
             lo, hi = 64 * c, 64 * c + 64
             o = v("pb7", lo, hi)
             mm(o, v("Im4k"), v("VL", lo, hi), True, False)
+            for q in range(16):
+                mm(o, v("LQh", 128 * q, 128 * q + 128), v("GV%d" % c, q, 1024, 16), False, False)
             mm(o, v("Im4k"), v("B3", lo, hi), False, False)
             for q in range(16):
-                mm(o, v("LQ1", 128 * q, 128 * q + 128), v("AE%d" % (c % 2), q, 1024, 16), False, q == 15)
+                mm(o, v("LQ1", 128 * q, 128 * q + 128), v("EE%d" % (c % 2), q, 1024, 16), False, q == 15)
 
-        send("LST", rL, to, "lR", "aR%d" % t)
+        par[0] = 0
+        sent = {}
+        sent["R"] = send("VNC", rL, to, "lR", "aR%d" % t)
+        masks()
+        sent["P"] = send("Pb", rP, to, "lP", "aP%d" % t)
         for w in MEASURE.split():
-            if t == 0 and w == "ss2":
-                consts3()
-            if t == 0 and w == "ee2":
-                consts4()
-            if w == "masks":
-                masks()
-                send("Pb", rP, to, "lP", "aP%d" % t)
-            else:
-                {"ss": ss, "gc": gc, "gv": gv, "dd": dd, "ab": ab, "ky": key, "pk": pick_a, "ee": ee, "ae": ae, "ds": ds}[w[:2]](int(w[2:]))
+            {"ss": ss, "gc": gc, "gv": gv, "dd": dd, "ab": ab, "ky": key, "pk": pick_a, "ee": ee, "ds": ds}[w[:2]](int(w[2:]))
         act(v("kb"), ind(v("SK"), v("bc15")))
-        ee(3)
-        ae(3)
-        send("Yn", rY, to, "lY", "aY%d" % t)
+        sent["Y"] = send("Y", rY, to, "lY", "aY%d" % t)
         for q in range(16):
-            mm(v("pb6", 0, 16), v("LW", 128 * q, 128 * q + 128), v("Yn", q, 256, 16), q == 0, q == 15)
-        ds(3)
+            mm(v("pb6", 16, 32), v("LQh", 128 * q, 128 * q + 128), v("Y", q, 256, 16), q == 0, q == 15)
+        for q in range(16):
+            mm(v("pb6", 0, 16), v("LW", 128 * q, 128 * q + 128), v("Y", q, 256, 16), q == 0, q == 15)
+        ts(v("Tl"), v("pb6", 16, 32), -1.0, OP.mult, v("lim"), OP.add)
+        wide("TB", "Tl")
         OH, O15, KV, K2 = v("pb0", 256, 512), v("pb1", 0, 256), v("pb1", 256, 512), v("pb2", 0, 256)
-        t1, t2 = v("pb3", 0, 256), v("pb3", 256, 512)
+        t1, SN, SC = v("pb2", 256, 512), v("pb3", 0, 256), v("pb0", 0, 256)
         act(v("pb2", 256, 512), v("Pb"))
-        act(v("Y"), v("Yn"), scale=-1.0)
         tt(OH, v("kb"), v("KS"), OP.is_equal)
         tt(v("m2"), v("V"), OH, OP.mult)
         tt(v("m3"), v("N"), OH, OP.mult)
         scan(v("m4"), v("RS"), v("m2"), OP.mult, OP.add)
         scan(v("m5"), v("RS"), v("m3"), OP.mult, OP.add)
         ts(v("K37"), last("m4"), 37.0, OP.mult)
+        kq = v("SB", 16, 32)
+        line(kq, v("kp2"), -1.0, 17.0)
         cp(v("UI"), v("pb6", 0, 16))
-        cp(v("VK"), last("m4"))
         ts(v("UI"), v("UI"), 4095, OP.bitwise_and)
-        cp(v("NK"), last("m5"))
         tt(v("HI"), v("UI"), v("UI"), OP.mult)
-        ts(v("kq"), v("kp2"), -1.0, OP.mult, 17.0, OP.add)
         ts(v("HI"), v("HI"), 5, OP.arith_shift_right)
-        cp(v("SB", 32, 48), last("m5"))
+        act(v("SB", 32, 48), last("m5"))
         tt(v("HI"), v("HI"), v("K37"), OP.add)
-        ts(v("SB", 16, 32), v("kp2"), -1.0, OP.mult, 17.0, OP.add)
         ts(v("HI"), v("HI"), 4095, OP.bitwise_and)
-        wide("NKB", "NK")
-        wide("VKB", "VK")
-        ts(v("rest"), v("kq"), 0.0, OP.is_equal)
-        ts(v("hm"), v("HI"), 16384.0, OP.subtract)
-        ts(v("s4"), v("HI"), 2.0, OP.add)
+        act(v("NKB"), ind(v("m5"), v("bc15")))
+        act(v("VKB"), ind(v("m4"), v("bc15")))
+        ts(v("rest"), v("kp2"), 17.0, OP.is_equal)
         F = v("pb0", 0, 256)
-        ts(F, v("pb7", 0, 256), v("lim"), OP.is_le)
+        tt(F, v("TB"), v("pb7", 0, 256), OP.is_ge)
         tt(v("m1"), F, v("PW"), OP.mult)
         scan(v("SM"), v("RS"), v("m1"), OP.mult, OP.max)
         ts(v("MX"), last("SM"), 12, OP.arith_shift_right)
         ts(v("VM"), last("SM"), 4095, OP.bitwise_and)
         ts(v("close"), v("MX"), 0.0, OP.is_gt)
-        tt(v("s1"), v("kq"), v("MX"), OP.subtract)
-        ts(v("s2"), v("MX"), 0.0, OP.is_equal)
+        tt(v("s1"), kq, v("MX"), OP.subtract)
         tt(v("SB", 0, 16), v("s1"), v("close"), OP.mult)
-        send("SB", rB, to, "lB", "aB%d" % t)
-        tt(v("grow"), v("s2"), v("live"), OP.mult)
-        tt(v("s4"), v("s4"), v("grow"), OP.mult)
-        ts(v("zL"), v("s4"), -1.0, OP.add)
-        tt(v("s7"), v("HI"), v("grow"), OP.mult)
-        ts(v("s6"), v("grow"), 16.0, OP.mult, -1.0, OP.add)
-        wide("s6B", "s6")
+        sent["B"] = send("SB", rB, to, "lB", "aB%d" % t)
+        tt(v("grow"), v("live"), v("close"), OP.subtract)
+        names("HI", "grow")
+        wide("s6B", "grow", 16.0, -1.0)
         tt(v("x"), v("s7"), v("VM"), OP.add)
 
         def gap1():
             wide("xB", "x")
-            tt(v("s8"), v("hm"), v("grow"), OP.mult)
             tt(v("s3"), v("nn"), v("grow"), OP.add)
-            ts(v("hp"), v("s8"), 16384.0, OP.add)
             ts(v("s3"), v("s3"), 16.0, OP.min)
             tt(O15, v("s6B"), v("pb2", 256, 512), OP.is_equal)
             tt(v("nn"), v("s3"), v("SB", 0, 16), OP.subtract)
@@ -513,18 +602,16 @@ def rank_program(g, core, T, topo):
         if not lastt:
             tt(v("m8"), v("xB"), OH, OP.mult)
             tt(v("m9"), v("NKB"), O15, OP.mult)
-            tt(t1, v("N"), K2, OP.mult)
-            tt(t2, t1, v("m8"), OP.add)
-            tt(v("N"), t2, v("m9"), OP.add)
-        tt(v("m6"), v("VKB"), O15, OP.mult)
-        tt(t1, v("C"), K2, OP.mult)
-        tt(t2, t1, v("m3"), OP.add)
-        tt(v("C"), t2, v("m6"), OP.add)
+            mm(SN, v("IdF"), v("m8"), True, False)
+            mm(SN, v("IdF"), v("m9"), False, False)
+        tt(v("nC"), v("VKB"), O15, OP.mult)
+        act(v("oC"), v("m3"))
         cp(v("cI"), v("pb6", 0, 1))
         ts(v("cI"), v("cI"), 31, OP.bitwise_and)
-        tt(v("lim"), v("thm"), v("cI"), OP.add)
+        ts(v("lim"), v("cI"), 0.5, OP.mult, v("thm"), OP.add)
         for m, b in (("R", rL), ("P", rP), ("Y", rY), ("B", rB)):
-            arrive(b, "a%s%d" % (m, t), frm)
+            arrive(b, "a%s%d" % (m, t), frm, sent[m])
+        par[0] = 1
         e_, k_, n_ = v(rB, 0, 16), v(rB, 16, 32), v(rB, 32, 48)
         tt(v("s1"), e_, v("nn"), OP.is_gt)
         tt(v("s2"), n_, v("V0"), OP.subtract)
@@ -538,36 +625,39 @@ def rank_program(g, core, T, topo):
         tt(v("s3"), v("s3"), v("take"), OP.mult)
         tt(v("V0"), v("V0"), v("s2"), OP.add)
         tt(v("nn"), v("nn"), v("s3"), OP.add)
-        ts(v("s4"), k_, 0.0, OP.is_gt)
-        ts(v("s6"), v("nn"), 1.0, OP.is_ge)
-        ts(v("s5"), v("V0"), 2.0, OP.add)
-        tt(v("s6"), v("s6"), v("s4"), OP.mult)
-        ts(v("hm"), v("V0"), 16384.0, OP.subtract)
-        tt(v("s5"), v("s5"), v("s6"), OP.mult)
+        act(v("s4"), k_, AF.Sign)
+        ts(v("s1"), v("nn"), 1.0, OP.is_ge)
+        tt(v("has"), v("s1"), v("s4"), OP.mult)
         cp(v("z16"), v("V0"))
-        ts(v("zL"), v("s5"), -1.0, OP.add)
+        names("V0", "has")
 
-        def take(own, k):
-            cp(t1, v(rL, 256 * k, 256 * k + 256))
-            tt(v("m2"), v(own), NT, OP.mult)
-            tt(t2, t1, v("TKb"), OP.mult)
-            tt(v(own), t2, v("m2"), OP.add)
+        def take(k, acc):
+            own = v("VNC", 256 * k, 256 * k + 256)
+            a, b = v("m%d" % (2 * k)), v("m%d" % (2 * k + 1))
+            tt(a, own, v("pb2", 0, 256), OP.mult)
+            tt(b, v(rL, 256 * k, 256 * k + 256), TP, OP.mult)
+            mm(acc, v("IdF"), a, False, False)
+            mm(acc, v("IdF"), b, False, True)
+            act(own, acc)
             if not lastt:
-                cp(v("LST", 256 * k, 256 * k + 256), v(own))
+                cp(v("LST", 256 * k, 256 * k + 256), acc)
 
         def gap3():
-            tt(v("s7"), v("take"), k_, OP.mult)
-            ts(v("s8"), v("take"), 16.0, OP.mult)
-            tt(v("MXe"), v("MXe"), v("s7"), OP.add)
-            tt(v("kqe"), v("kq"), v("s8"), OP.add)
+            tt(t1, v("V"), NT, OP.mult)
+            tt(v("m1"), v(rL, 0, 256), TP, OP.mult)
+            tt(v("V"), t1, v("m1"), OP.add)
+            if not lastt:
+                cp(v("LST", 0, 256), v("V"))
+            tt(K2, K2, v("TKb"), OP.subtract)
+            tt(v("s2"), v("take"), k_, OP.mult)
+            line(v("s3"), v("take"), 16.0, 0.0)
+            tt(v("MXe"), v("MXe"), v("s2"), OP.add)
+            tt(v("kqe"), kq, v("s3"), OP.add)
             wide("MXB", "MXe")
             wide("kqB", "kqe")
-            act(v("kthB"), v("kqB"), AF.Identity, scale=-1.0, bias=15.0)
-            act(v("mthB"), v("MXB"), AF.Identity, scale=-1.0, bias=16.0)
-            take("V", 0)
+            line(v("kthB"), v("kqB"), -1.0, 15.0)
+            line(v("mthB"), v("MXB"), -1.0, 16.0)
             limits()
-            tt(v("s7"), v("hm"), v("s6"), OP.mult)
-            ts(v("hp"), v("s7"), 16384.0, OP.add)
 
         def gap4():
             tt(v("Pa"), v("Pb"), NT, OP.mult)
@@ -575,11 +665,11 @@ def rank_program(g, core, T, topo):
             PS = v("pb6", 0, 256)
             mm(PS, v("Ident"), v("Pa"), True, False)
             mm(PS, v("Ident"), v("Pr"), False, True)
-            tt(v("BL"), ind(v("X", 0, W), v("z16")), v(rY), OP.subtract)
+            tt(v("BL"), ind(v("X", 0, W), v("z16")), v(rY), OP.add)
             ts(v("BL2"), v("BL"), 0.5, OP.mult, 159.75, OP.add)
             ts(v("BL"), v("BL2"), -160.0, OP.add)
             if not lastt:
-                take("N", 1)
+                take(1, SN)
 
         dedupe("zL", gap3, gap4)
         cp(ind(v("X"), v("off16")), v("BL"))
@@ -588,7 +678,9 @@ def rank_program(g, core, T, topo):
             dma("S", T.yx[:, half:W], T.X[:, half:W], [v("X", half, W)], [])
         else:
             gv(0)
-        take("C", 2)
+        mm(SC, v("IdF"), v("oC"), True, False)
+        mm(SC, v("IdF"), v("nC"), False, False)
+        take(2, SC)
         PS, ga, gb = v("pb6", 0, 256), v("pb2", 0, 256), v("pb2", 256, 512)
         tt(ga, v("kthB"), PS, OP.is_lt)
         tt(gb, v("mthB"), PS, OP.is_le)
@@ -598,7 +690,6 @@ def rank_program(g, core, T, topo):
         mm(PP, v("Ident"), v("Pr"), False, False)
         mm(PP, v("Ident"), v("g1"), False, False)
         mm(PP, v("In1"), v("g2"), False, True)
-        cp(v("Pb"), PP)
 
     tt(v("Hx"), bc(v("nn")), v("DG"), OP.mult)
     op("T", lambda e: e.matmul(T.pb4[0:8, 0:256], T.G8T[:], v("Hx")[0], True, True), [v("G8T"), v("Hx")], [v("pb4", 0, 256)])
@@ -625,9 +716,11 @@ def rank_program(g, core, T, topo):
     ts(v("IV"), v("iw"), 12, OP.arith_shift_right)
     ts(v("IC"), v("iw"), 4095, OP.bitwise_and)
     cp(v("V"), v("IV"))
-    dma("Y", T.yv[:], T.V[:], [v("V")], [])
+    dma("Y", T.yv[:], v("V")[0], [v("V")], [])
     cp(v("C"), v("IC"))
-    dma("S", T.yc[:], T.C[:], [v("C")], [])
+    dma("S", T.yc[:], v("C")[0], [v("C")], [])
+    for i in order():
+        OPS[i][1](OPS[i][2], OPS[i][3])
     for s in sorted(count):
         if known["G"].get(s, 0) < count[s]:
             g.wait_ge(T.sem[s], count[s])

@@ -6,10 +6,10 @@ W, L, S, ST = 4096, 256, 16, 5
 BIG = 8388608.0
 F32, BF, I32, U16 = "float32", "bfloat16", "int32", "uint16"
 
-MEASURE = ("gc0 ss0 gv1 ss1 dd0 ab0 ky0 pk0 gc1 dd1 gv2 ee0 ab1 ss2 ky1 gc2 dd2 gv3 ab2 ds0 gc3 "
-           "pk1 ky2 ee1 ss3 pk2 ds1 ee2 dd3 ab3 ky3 ds2 pk3 ee3 ds3")
-CYC, GATHER, SCATTER, WAKE, SLACK = 0.001, 1.5, 3.8, 0.08, 0.02
-BETA = 0.1
+MEASURE = ("gc0 ss0 dd0 gv1 ab0 ky0 ss1 gc1 dd1 pk0 ee0 gv2 ab1 ky1 ss2 gc2 dd2 pk1 ds0 ee1 "
+           "gv3 ab2 ky2 ss3 gc3 dd3 pk2 ds1 ee2 ab3 ky3 pk3 ds2 ee3 ds3")
+CYC, GATHER, SCATTER, WAKE, SLACK = 0.001, 1.5, 3.8, 0.18, 0.02
+BETA = 0.03
 SCRATCH = {"X": ("sbuf", [128, W + L], BF)}
 ALIAS = {}
 
@@ -38,7 +38,7 @@ _add("Pb Vg VL B3 Y Yn SYs GYs BL BL2 Pa Pr g1 g2", 256, BF)
 _add("LST", 768, U16)
 _pack("RR", "Ru Ru'", 256, U16)
 _pack("EQQ", "EQ EQ'", 2176, BF)
-_pack("PLF", "nn V0 live kq kp2 VK NK ng nl close grow gsel rest MXe TR hm hp cnt s1 s2 s3 s4 s5 s6 s7 s8 s9 zL take kqe mth kth x Tl "
+_pack("PLF", "nn V0 live kp2 H2 Z0 Z1 close grow rest MXe TR hp s1 s2 s3 s4 s5 s6 s7 s8 s9 zL take kqe mth kth x Tl "
       "s1' s2' s3' s4' s5' s6' s7' s8' s9' hp' zL' has", 16, F32)
 _pack("PLI", "KA KB UI HI K37 MX VM", 16, I32)
 _pack("PLU", "o16 off16 z16 bcA bc15", 16, U16)
@@ -317,7 +317,7 @@ def rank_program(g, core, T, topo):
     iota(v("mm"), [[1, 128]], 0, 0)
     iota(v("cc"), [[1, 64]], 0, 0)
     iota(v("bcI"), [[16, 4], [0, 16]], 0, 0)
-    iota(v("f2", 0, 16), [[16, 16]], W + 1, 0)
+    iota(v("f2", 0, 16), [[16, 16]], W + 2, 0)
     ts(v("pmI"), v("pcI"), 15, OP.bitwise_and)
     ts(v("p4I"), v("pcI"), 4, OP.arith_shift_right)
     ts(v("btI"), v("p4I"), 1, OP.bitwise_and)
@@ -328,15 +328,15 @@ def rank_program(g, core, T, topo):
     cp(v("bc15"), v("iw", 16, 32))
 
     def conv(src, dst):
+        act(v("CIN2", 0, 240), v(src, 16, 256))
+        act(v("CIN2", 240, 256), v(src, 0, 16))
         tr(v("CT1"), v(src))
-        cp(v("CIN2", 0, 240), v(src, 16, 256))
-        cp(v("CIN2", 240, 256), v(src, 0, 16))
         tr(v("CT2"), v("CIN2"))
-        cp(v("CT3", 16, 256), v("CT2", 0, 240))
-        cp(v("CT3", 0, 16), v("CT2", 240, 256))
-        tt(v("m8"), v("CT1"), v("CT3"), OP.subtract)
-        tt(v("m9"), v("m8"), v("MP"), OP.mult)
-        tt(v(dst), v("m9"), v("CT3"), OP.add)
+        act(v("pb6", 16, 256), v("CT2", 0, 240))
+        act(v("pb6", 0, 16), v("CT2", 240, 256))
+        tt(v("pb5", 0, 256), v("CT1"), v("pb6", 0, 256), OP.subtract)
+        tt(v("m9"), v("pb5", 0, 256), v("MP"), OP.mult)
+        tt(v(dst), v("m9"), v("pb6", 0, 256), OP.add)
 
     ts(v("m1"), v("IV"), 4096.0, OP.mult)
     tt(v("VCA"), v("m1"), v("IC"), OP.add)
@@ -354,7 +354,7 @@ def rank_program(g, core, T, topo):
         cp(v("C"), v("IC"))
         cp(v("N", 0, 255), v("V", 1, 256))
         cp(v("N", 255, 256), v("V", 255, 256))
-        cp(v("V0"), v("V", 0, 256, 16))
+        ts(v("V0"), v("V", 0, 256, 16), 2.0, OP.add)
         ts(v("DG"), v("QC"), v("pmF"), OP.is_equal)
         ts(v("RS"), v("QC"), 0.0, OP.is_gt)
         op("V", lambda e: e.tensor_scalar(T.G8[0:8, :], T.mg[0:8, :], v("pcF", p=8)[0], None, OP.is_equal), [v("mg"), v("pcF")], [v("G8")])
@@ -392,7 +392,7 @@ def rank_program(g, core, T, topo):
         ts(v("LQh"), v("LQ1"), -0.5, OP.mult)
         cp(v("wF"), v("WI"))
         ts(v("LW"), v("LQ1"), v("wF"), OP.mult)
-        ts(v("LM"), v("QC"), v("pmF"), OP.is_gt)
+        ts(v("LM"), v("QC"), v("pmF"), OP.is_le, -16384.0, OP.mult)
         ts(v("blk"), v("mg"), v("p4F"), OP.is_equal)
         ts(v("blk8k"), v("blk"), 8192.0, OP.mult)
         fill(v("onesF"), 1.0)
@@ -408,7 +408,7 @@ def rank_program(g, core, T, topo):
     PP = v("pb7", 0, 256)
 
     def masks():
-        act(v("m1"), PP, AF.Identity, scale=-4096.0, bias=65536.0)
+        act(v("m1"), PP, AF.Identity, scale=-8192.0, bias=131074.0)
         act(v("Pb"), PP)
         tt(v("Vg"), v("ngB"), PP, OP.is_ge)
         tt(v("VL"), v("nlB"), PP, OP.is_ge)
@@ -419,7 +419,7 @@ def rank_program(g, core, T, topo):
         wide("zb", z)
         mm(v("pb4", 0, 256), v("blkF"), v("Hx"), True, True)
         gap1()
-        tt(v("pb0", 0, 256), v("pb4", 0, 256), v("LM"), OP.mult)
+        tt(v("pb0", 0, 256), v("pb4", 0, 256), v("LM"), OP.add)
         cp(v("Ru"), v("pb4", 0, 256))
         tt(v("EQ", 0, 256), v("zb"), v("pb0", 0, 256), OP.is_equal)
         mm(v("pb5", 0, 256), v("blk8k"), v("EQ", 0, 256), True, False)
@@ -434,13 +434,10 @@ def rank_program(g, core, T, topo):
         scan(v("f2"), v("RS"), v("f1"), OP.mult, OP.add)
         tt(v("s5"), last("f2"), v("hp"), OP.add)
         tt(v("s8"), v("s5"), v("TR"), OP.min)
-        ts(v("off16"), v("s8"), -1.0, OP.add)
+        ts(v("off16"), v("s8"), -2.0, OP.add)
 
-    def names(z, yes):
-        tt(v("s7"), v(z), v(yes), OP.mult)
-        line(v("s9"), v(yes), 2.0, -1.0)
+    def names(yes):
         line(v("s6"), v(yes), -16384.0, 16384.0)
-        tt(v("zL"), v("s7"), v("s9"), OP.add)
         tt(v("hp"), v("s6"), v("zL"), OP.add)
 
     def send(buf, dst_buf, dst_rank, lsem, asem):
@@ -464,7 +461,7 @@ def rank_program(g, core, T, topo):
         add("F", emit, [], [v(buf)], 0.0, 1.0, [sent])
 
     def gv(c):
-        act(v("GV%d" % c), ind(v("X", 0, W), v("LST", 64 * c, 64 * c + 64)))
+        (cp if c == 0 else act)(v("GV%d" % c), ind(v("X", 0, W), v("LST", 64 * c, 64 * c + 64)))
 
     gv(0)
     consts1()
@@ -544,7 +541,7 @@ def rank_program(g, core, T, topo):
         ts(v("Tl"), v("pb6", 16, 32), -1.0, OP.mult, v("lim"), OP.add)
         wide("TB", "Tl")
         OH, O15, KV, K2 = v("pb0", 256, 512), v("pb1", 0, 256), v("pb1", 256, 512), v("pb2", 0, 256)
-        t1, SN, SC = v("pb2", 256, 512), v("pb3", 0, 256), v("pb0", 0, 256)
+        t1, SN, SC, PS = v("pb2", 256, 512), v("pb3", 0, 256), v("pb6", 0, 256), v("pb0", 0, 256)
         act(v("pb2", 256, 512), v("Pb"))
         tt(OH, v("kb"), v("KS"), OP.is_equal)
         tt(v("m2"), v("V"), OH, OP.mult)
@@ -558,9 +555,10 @@ def rank_program(g, core, T, topo):
         ts(v("UI"), v("UI"), 4095, OP.bitwise_and)
         tt(v("HI"), v("UI"), v("UI"), OP.mult)
         ts(v("HI"), v("HI"), 5, OP.arith_shift_right)
-        act(v("SB", 32, 48), last("m5"))
+        line(v("SB", 32, 48), last("m5"), 1.0, 2.0)
         tt(v("HI"), v("HI"), v("K37"), OP.add)
         ts(v("HI"), v("HI"), 4095, OP.bitwise_and)
+        ts(v("H2"), v("HI"), 2.0, OP.add)
         act(v("NKB"), ind(v("m5"), v("bc15")))
         act(v("VKB"), ind(v("m4"), v("bc15")))
         ts(v("rest"), v("kp2"), 17.0, OP.is_equal)
@@ -568,19 +566,20 @@ def rank_program(g, core, T, topo):
         tt(F, v("TB"), v("pb7", 0, 256), OP.is_ge)
         tt(v("m1"), F, v("PW"), OP.mult)
         scan(v("SM"), v("RS"), v("m1"), OP.mult, OP.max)
-        ts(v("MX"), last("SM"), 12, OP.arith_shift_right)
-        ts(v("VM"), last("SM"), 4095, OP.bitwise_and)
-        ts(v("close"), v("MX"), 0.0, OP.is_gt)
+        ts(v("close"), last("SM"), 0.0, OP.is_gt)
+        ts(v("MX"), last("SM"), 13, OP.arith_shift_right)
+        ts(v("VM"), last("SM"), 8191, OP.bitwise_and)
         tt(v("s1"), kq, v("MX"), OP.subtract)
         tt(v("SB", 0, 16), v("s1"), v("close"), OP.mult)
         sent["B"] = send("SB", rB, to, "lB", "aB%d" % t)
         tt(v("grow"), v("live"), v("close"), OP.subtract)
-        names("HI", "grow")
+        tt(v("zL"), v("H2"), v("grow"), OP.mult)
+        names("grow")
         wide("s6B", "grow", 16.0, -1.0)
-        tt(v("x"), v("s7"), v("VM"), OP.add)
+        tt(v("x"), v("zL"), v("VM"), OP.add)
 
         def gap1():
-            wide("xB", "x")
+            wide("xB", "x", 1.0, -2.0)
             tt(v("s3"), v("nn"), v("grow"), OP.add)
             ts(v("s3"), v("s3"), 16.0, OP.min)
             tt(O15, v("s6B"), v("pb2", 256, 512), OP.is_equal)
@@ -605,17 +604,27 @@ def rank_program(g, core, T, topo):
             mm(SN, v("IdF"), v("m8"), True, False)
             mm(SN, v("IdF"), v("m9"), False, False)
         tt(v("nC"), v("VKB"), O15, OP.mult)
-        act(v("oC"), v("m3"))
         cp(v("cI"), v("pb6", 0, 1))
         ts(v("cI"), v("cI"), 31, OP.bitwise_and)
         ts(v("lim"), v("cI"), 0.5, OP.mult, v("thm"), OP.add)
+        mm(SC, v("IdF"), v("m3"), True, False)
+        mm(SC, v("IdF"), v("nC"), False, False)
         for m, b in (("R", rL), ("P", rP), ("Y", rY), ("B", rB)):
             arrive(b, "a%s%d" % (m, t), frm, sent[m])
         par[0] = 1
         e_, k_, n_ = v(rB, 0, 16), v(rB, 16, 32), v(rB, 32, 48)
+        act(v("s4"), k_, AF.Sign)
         tt(v("s1"), e_, v("nn"), OP.is_gt)
-        tt(v("s2"), n_, v("V0"), OP.subtract)
+        ts(v("s7"), v("nn"), 1.0, OP.is_ge)
+        tt(v("s9"), v("s7"), v("s4"), OP.mult)
+        tt(v("Z0"), v("V0"), v("s9"), OP.mult)
+        tt(v("Z1"), n_, v("Z0"), OP.subtract)
         tt(v("take"), v("s1"), v("rest"), OP.mult)
+        tt(v("Z1"), v("Z1"), v("take"), OP.mult)
+        tt(v("zL"), v("Z0"), v("Z1"), OP.add)
+        tt(v("has"), v("s9"), v("take"), OP.max)
+        names("has")
+        tt(v("s2"), n_, v("V0"), OP.subtract)
         tt(v("s3"), e_, v("nn"), OP.subtract)
         wide("TKb", "take")
         act(v("pb1", 0, 256), v("TKb"))
@@ -625,11 +634,7 @@ def rank_program(g, core, T, topo):
         tt(v("s3"), v("s3"), v("take"), OP.mult)
         tt(v("V0"), v("V0"), v("s2"), OP.add)
         tt(v("nn"), v("nn"), v("s3"), OP.add)
-        act(v("s4"), k_, AF.Sign)
-        ts(v("s1"), v("nn"), 1.0, OP.is_ge)
-        tt(v("has"), v("s1"), v("s4"), OP.mult)
-        cp(v("z16"), v("V0"))
-        names("V0", "has")
+        ts(v("z16"), v("V0"), -2.0, OP.add)
 
         def take(k, acc):
             own = v("VNC", 256 * k, 256 * k + 256)
@@ -662,14 +667,12 @@ def rank_program(g, core, T, topo):
         def gap4():
             tt(v("Pa"), v("Pb"), NT, OP.mult)
             tt(v("Pr"), v(rP), TP, OP.mult)
-            PS = v("pb6", 0, 256)
-            mm(PS, v("Ident"), v("Pa"), True, False)
-            mm(PS, v("Ident"), v("Pr"), False, True)
             tt(v("BL"), ind(v("X", 0, W), v("z16")), v(rY), OP.add)
             ts(v("BL2"), v("BL"), 0.5, OP.mult, 159.75, OP.add)
             ts(v("BL"), v("BL2"), -160.0, OP.add)
             if not lastt:
                 take(1, SN)
+            take(2, SC)
 
         dedupe("zL", gap3, gap4)
         cp(ind(v("X"), v("off16")), v("BL"))
@@ -678,10 +681,9 @@ def rank_program(g, core, T, topo):
             dma("S", T.yx[:, half:W], T.X[:, half:W], [v("X", half, W)], [])
         else:
             gv(0)
-        mm(SC, v("IdF"), v("oC"), True, False)
-        mm(SC, v("IdF"), v("nC"), False, False)
-        take(2, SC)
-        PS, ga, gb = v("pb6", 0, 256), v("pb2", 0, 256), v("pb2", 256, 512)
+        mm(PS, v("Ident"), v("Pa"), True, False)
+        mm(PS, v("Ident"), v("Pr"), False, True)
+        ga, gb = v("pb2", 0, 256), v("pb2", 256, 512)
         tt(ga, v("kthB"), PS, OP.is_lt)
         tt(gb, v("mthB"), PS, OP.is_le)
         tt(v("g1"), v("MXB"), ga, OP.mult)
@@ -694,23 +696,19 @@ def rank_program(g, core, T, topo):
     tt(v("Hx"), bc(v("nn")), v("DG"), OP.mult)
     op("T", lambda e: e.matmul(T.pb4[0:8, 0:256], T.G8T[:], v("Hx")[0], True, True), [v("G8T"), v("Hx")], [v("pb4", 0, 256)])
     ts(v("m7"), v("V"), 4096.0, OP.mult)
-    tt(v("VCA"), v("m7"), v("C"), OP.add)
+    VC = v("pb2", 0, 256)
+    tt(VC, v("m7"), v("C"), OP.add)
     tt(v("pb3", 0, 256), v("nlB"), PP, OP.is_ge)
-    ts(v("m6"), v("pb3", 0, 256), -100.0, OP.mult, 100.0, OP.add)
-    tt(v("m1"), PP, v("m6"), OP.add)
+    line(v("m6"), v("pb3", 0, 256), -100.0, 100.0)
+    tt(v("Pa"), PP, v("m6"), OP.add)
     op("V", lambda e: e.tensor_copy(T.LNF[0:8, :], T.pb4[0:8, 0:256]), [v("pb4", 0, 256)], [v("LNF")])
     dma("Y", T.yn[:], T.LNF[0:8, :], [v("LNF")], [])
-    for p in range(0, 16, 2):
-        bs = v("pb%d" % (2 + p // 2 % 2), 0, 256)
-        ts(v("pb%d" % (p // 2 % 2), 0, 256), v("m1"), float(p), OP.is_equal)
-        for j in range(2):
-            b = v("pb%d" % (p // 2 % 2), 0, 256)
-            if j == 1:
-                ts(b, v("m1"), float(p + 1), OP.is_equal)
-            pr, sn = v("m%d" % (2 + (p + j) % 3)), "m%d" % (5 + (p + j) % 3) if (p + j) % 3 != 1 else "f2"
-            tt(pr, b, v("VCA"), OP.mult)
-            scan(v(sn), v("RS"), pr, OP.mult, OP.add)
-            act(v("SO", p + j, 256, 16), last(sn))
+    for p in range(16):
+        b, pr, sn = v(("g1", "g2", "Pr")[p % 3]), v("m%d" % (2 + p % 3)), ("m5", "m7", "m8")[p % 3]
+        ts(b, v("Pa"), float(p), OP.is_equal)
+        tt(pr, b, VC, OP.mult)
+        scan(v(sn), v("RS"), pr, OP.mult, OP.add)
+        act(v("SO", p, 256, 16), last(sn))
     conv("SO", "VCB")
     cp(v("iw"), v("VCB"))
     ts(v("IV"), v("iw"), 12, OP.arith_shift_right)

from concourse.mybir import AluOpType, AxisListType, ActivationFunctionType

OP = AluOpType
AF = ActivationFunctionType
W, L, S, ST = 4096, 256, 16, 5
BIG = 8388608.0
F32, BF, I32, U16 = "float32", "bfloat16", "int32", "uint16"

MEASURE = ("gc0 ss0 dd0 gv1 ab0 ky0 ss1 gc1 dd1 pk0 ee0 gv2 ab1 ky1 ss2 gc2 dd2 pk1 ds0 ee1 "
           "gv3 ab2 ky2 ss3 gc3 dd3 pk2 ds1 ee2 ab3 ky3 pk3 ds2 ee3 ds3")
CYC, GATHER, SCATTER, WAKE, SLACK = 0.001, 1.5, 3.8, 0.18, 0.02
BETA = 0.03
SCRATCH = {"X": ("sbuf", [128, W + L], BF)}
ALIAS = {}


def _pack(buf, names, cols, d):
    names = names.split()
    for k, n in enumerate(names):
        ALIAS[n] = (buf, k * cols, cols, d)
    SCRATCH[buf] = ("sbuf", [128, len(names) * cols], d)


def _add(names, cols, d):
    for n in names.split():
        SCRATCH[n] = ("sbuf", [128, cols], d)


for _c in range(4):
    _add("GV%d SS%d GC%d" % (_c, _c, _c), 1024, BF)
_add("AB0 AB1 EE0 EE1", 1024, BF)
_pack("VNC", "V N C", 256, F32)
_add("VCB CIN2 CT1 CT2 DG", 256, F32)
_pack("MF", "PW m1 m2 m3 m4 m5 m6 m7 m8 m9 KS LM RS MP CT3 QC Hx f1 f2 SO VCA kb s6B zb xB NKB VKB TKb kthB mthB MXB kqB ngB nlB KVs TB nC oC "
      "m1' m2' m3' m4' m5' m6' m7' m8' m9' Hx' f1' f2' zb'", 256, F32)
_add("SK SM IV IC iw LNI", 256, I32)
_add("Pb Vg VL B3 Y Yn SYs GYs BL BL2 Pa Pr g1 g2", 256, BF)
_add("LST", 768, U16)
_pack("RR", "Ru Ru'", 256, U16)
_pack("EQQ", "EQ EQ'", 2176, BF)
_pack("PLF", "nn V0 live kp2 H2 Z0 Z1 close grow rest MXe TR hp s1 s2 s3 s4 s5 s6 s7 s8 s9 zL take kqe mth kth x Tl "
      "s1' s2' s3' s4' s5' s6' s7' s8' s9' hp' zL' has", 16, F32)
_pack("PLI", "KA KB UI HI K37 MX VM", 16, I32)
_pack("PLU", "o16 off16 z16 bcA bc15", 16, U16)
_add("bcY", 64, U16)
_pack("COF", "pcF pmF p4F btF thm lim cs1 e1 e2 wF ws", 1, F32)
_pack("COI", "pcI pmI p4I btI cI", 1, I32)
_add("WI THI", 1, I32)
_add("mq mg mm blkF onesF G8 IdF", 128, F32)
_pack("IDS", "Ident In1 In2 Ibig Im256 Im4k ones blk blk8k", 128, BF)
_add("LQ1 LQk LQh LW", 2048, BF)
_add("CR", 64, BF)
_add("cc", 64, F32)
_add("LNF THF", 256, F32)
_add("G8T", 8, F32)
_add("bcI", 64, I32)
for _t in range(ST):
    _add("rL%d" % _t, 768, F32)
    _add("rP%d rY%d" % (_t, _t), 256, BF)
    _add("rB%d" % _t, 48, F32)
_add("SB", 48, F32)
for _b in range(8):
    SCRATCH["pb%d" % _b] = ("psum", [128, 512], F32)

SEMAPHORES = ["sV", "sS", "sT", "sG", "lR", "lP", "lY", "lB"]
SEMAPHORES += ["a%s%d" % (m, t) for m in "RPYB" for t in range(ST)]
SEMAPHORES += ["d%d" % k for k in range(24)]


def rank_program(g, core, T, topo):
    rank = T.rank_of(core)
    if rank is None:
        return
    queues = {"V": g.vector, "S": g.scalar, "T": g.tensor, "G": g, "Y": g.sync}
    count = {}
    known = {q: {} for q in queues}
    clock = {}
    recs = {}
    ndma = [0]

    par = [0]

    def v(name, lo=0, hi=None, step=1, p=None):
        if par[0] and name + "'" in ALIAS:
            name += "'"
        if name in ALIAS:
            name, at, width, _d = ALIAS[name]
            hi = at + (width if hi is None else hi)
            lo += at
        hi = SCRATCH[name][1][1] if hi is None else hi
        t = T[name]
        sl = slice(lo, hi, step) if step != 1 else slice(lo, hi)
        return (t[:, sl] if p is None else t[0:p, sl], [(name, lo, hi)], (hi - lo + step - 1) // step, False)

    def ind(win, off):
        return (win[0].indirect(off[0]), win[1] + off[1], off[2] * 16, True)

    def need(q, reads, writes):
        toks = []
        for acc, wr in [(a, False) for a in reads] + [(a, True) for a in writes]:
            name, lo, hi = acc
            bank = name.startswith("pb")
            for (l2, h2, tok, q2, w2) in recs.get(name, []):
                if bank and q2 != q:
                    toks.append(tok)
                elif lo < h2 and l2 < hi and (wr or w2):
                    if q2 == q and q == "T":
                        continue
                    toks.append(tok)
        return toks

    def wait(q, toks):
        best = {}
        for s, n in toks:
            best[s] = max(best.get(s, 0), n)
        kn = known[q]
        todo = sorted(best.items(), key=lambda a: -len(clock.get(a, {})))
        for s, n in todo:
            if kn.get(s, 0) >= n:
                continue
            if any(clock.get((s2, n2), {}).get(s, 0) >= n for s2, n2 in todo if s2 != s and kn.get(s2, 0) < n2):
                continue
            queues[q].wait_ge(T.sem[s], n)
            for s3, n3 in clock.get((s, n), {}).items():
                kn[s3] = max(kn.get(s3, 0), n3)
            kn[s] = max(kn.get(s, 0), n)

    def record(q, tok, reads, writes):
        for acc, wr in [(a, False) for a in reads] + [(a, True) for a in writes]:
            name, lo, hi = acc
            old = recs.get(name, [])
            if name.startswith("pb"):
                old = [r for r in old if r[3] == q]
            if wr:
                old = [r for r in old if not (lo <= r[0] and r[1] <= hi)]
            else:
                old = [r for r in old if r[4] or r[3] != q or (r[0], r[1]) != (lo, hi)]
            old.append((lo, hi, tok, q, wr))
            recs[name] = old

    def bump(q, sem, n):
        count[sem] = count.get(sem, 0) + n
        tok = (sem, count[sem])
        clock[tok] = dict(known[q])
        return tok

    OPS = []

    def add(q, emit, reads, writes, cost, lat=0.0, after=()):
        OPS.append([q, emit, [a for x in reads for a in x[1]], [a for x in writes for a in x[1]], cost, lat, list(after)])
        return len(OPS) - 1

    def op(q, fn, reads, writes, cost=0.06):
        def emit(rd, wr):
            wait(q, need(q, rd, wr))
            sem = "s" + q
            fn(queues[q]).then_inc(T.sem[sem], 1)
            record(q, bump(q, sem, 1), rd, wr)
        return add(q, emit, reads, writes, cost)

    def dma(q, out, in_, reads=(), writes=()):
        sem = "d%d" % ndma[0]
        ndma[0] += 1

        def emit(rd, wr):
            wait(q, need(q, rd, wr))
            queues[q].dma_start(out, in_).then_inc(T.sem[sem], 16)
            record(q + "d", bump(q, sem, 16), rd, wr)
        return add(q, emit, reads, writes, 0.1, 5.0 if writes and writes[0][1][0][0] == "X" else 2.2)

    def order():
        seen, deps, succ = {}, [], [[] for _ in OPS]
        for i, o in enumerate(OPS):
            q, dp = o[0], {}
            for j in o[6]:
                dp[j] = 1
            for acc, wr in [(a, 0) for a in o[2]] + [(a, 1) for a in o[3]]:
                name, lo, hi = acc
                bank = name.startswith("pb")
                if bank and seen.get(name) and seen[name][0][3] != q:
                    seen[name, "before"] = seen.pop(name)
                for r in seen.get((name, "before"), []):
                    dp[r[2]] = 1
                for (l2, h2, j, q2, w2) in seen.get(name, []):
                    if bank and q == "T":
                        dp[j] = max(dp.get(j, 0), 0)
                    elif lo < h2 and l2 < hi and (wr or w2):
                        dp[j] = 1
            for acc, wr in [(a, 0) for a in o[2]] + [(a, 1) for a in o[3]]:
                name, lo, hi = acc
                old = seen.get(name, [])
                if wr:
                    old = [r for r in old if not (lo <= r[0] and r[1] <= hi)]
                seen[name] = old + [(lo, hi, i, q, wr)]
            dp.pop(i, None)
            deps.append(dp)
            for j in dp:
                succ[j].append(i)
        n = len(OPS)
        prio = [0.0] * n
        for i in range(n - 1, -1, -1):
            prio[i] = OPS[i][4] + OPS[i][5] + max([prio[j] + (WAKE if deps[j][i] else -OPS[i][4]) for j in succ[i]] or [0.0])
        left = [len(dp) for dp in deps]
        start, fin = [0.0] * n, [0.0] * n
        free, ready, out = {}, {}, []

        def push(i):
            r = 0.0
            for j, k in deps[i].items():
                r = max(r, fin[j] + WAKE if k else start[j])
            ready.setdefault(OPS[i][0], []).append((r, BETA * i - prio[i], i))
        for i in range(n):
            if left[i] == 0:
                push(i)
        while len(out) < n:
            best = None
            for q, lst in ready.items():
                if lst:
                    t0 = max(free.get(q, 0.0), min(lst)[0])
                    p, i, r = min((c[1], c[2], c) for c in lst if c[0] <= t0 + SLACK)
                    st = max(t0, r[0])
                    if best is None or st < best[0]:
                        best = (st, q, i, r)
            st, q, i, r = best
            ready[q].remove(r)
            start[i] = st
            fin[i] = st + OPS[i][4] + OPS[i][5]
            free[q] = st + OPS[i][4]
            out.append(i)
            for j in succ[i]:
                left[j] -= 1
                if left[j] == 0:
                    push(j)
        return out

    def vcost(out, a, b=None):
        views = [x for x in (out, a, b) if x is not None]
        if out[3]:
            return 0.06 + SCATTER * CYC * out[2]
        if any(x[3] for x in views):
            return 0.06 + GATHER * CYC * out[2]
        n = max(out[2], a[2])
        psum = any(x[1][0][0].startswith("pb") for x in views[1:])
        small = all(SCRATCH[x[1][0][0]][2] in (BF, U16) for x in views)
        if b is not None:
            n *= 1 if psum else 2
        elif small:
            n *= 0.5
        return max(64, n) * CYC

    def tt(out, a, b, o):
        op("V", lambda e: e.tensor_tensor(out[0], a[0], b[0], o), [a, b], [out], vcost(out, a, b))

    def ts(out, a, s1, o0, s2=None, o1=None):
        rd = [a] + [x for x in (s1, s2) if isinstance(x, tuple)]
        x1 = s1[0] if isinstance(s1, tuple) else s1
        x2 = s2[0] if isinstance(s2, tuple) else s2
        if o1 is None:
            op("V", lambda e: e.tensor_scalar(out[0], a[0], x1, None, o0), rd, [out], vcost(out, a))
        else:
            op("V", lambda e: e.tensor_scalar(out[0], a[0], x1, x2, o0, o1), rd, [out], vcost(out, a))

    def cp(out, a):
        op("V", lambda e: e.tensor_copy(out[0], a[0]), [a], [out], vcost(out, a))

    def act(out, a, f=AF.Copy, scale=1.0, bias=0.0):
        c = (0.07 + GATHER * CYC * out[2]) if a[3] else 0.06 + CYC * max(64, out[2])
        op("S", lambda e: e.activation(out[0], a[0], f, bias=bias, scale=scale), [a], [out], c)

    def mm(out, l, r, start, stop):
        c = max(64, r[2]) * CYC * (4 if SCRATCH[r[1][0][0]][2] == F32 else 1)
        op("T", lambda e: e.matmul(out[0], l[0], r[0], start, stop), [l, r], [out], c)

    def scan(out, d0, d1, o0, o1):
        op("V", lambda e: e.tensor_tensor_scan(out[0], d0[0], d1[0], 0.0, o0, o1), [d0, d1], [out], max(64, out[2]) * CYC)

    def tr(out, a):
        op("V", lambda e: e.transpose(out[0], a[0]), [a], [out], vcost(out, a))

    def fill(out, c):
        op("V", lambda e: e.memset(out[0], c), [], [out])

    def iota(out, pat, base, cm):
        if SCRATCH[out[1][0][0]][2] == I32:
            op("G", lambda e: e.iota(out[0], pat, base, cm), [], [out], 0.13 + 2 * CYC * out[2])
        else:
            op("G", lambda e: e.iota(out[0], pat, base, cm, allow_small_or_imprecise_dtypes=True), [], [out], 0.13 + 2 * CYC * out[2])

    def bc(x):
        return ind(x, v("bcA"))

    def wide(dst, x, scale=1.0, bias=0.0):
        act(v(dst), bc(v(x)), AF.Copy if (scale, bias) == (1.0, 0.0) else AF.Identity, scale, bias)

    def line(dst, x, scale, bias):
        act(dst, x, AF.Identity, scale, bias)

    def last(name, a0=0, a1=16):
        return v(name, a0 * 16 + 15, a1 * 16, 16)

    half = W // 2
    dma("Y", T.IV[:], T.vl[:], [], [v("IV")])
    dma("S", T.IC[:], T.cl[:], [], [v("IC")])
    dma("Y", T.X[:, 0:half], T.xc[:, 0:half], [], [v("X", 0, half)])
    dma("S", T.X[:, half:W], T.xc[:, half:W], [], [v("X", half, W)])
    dma("Y", T.LNI[0:8, :], T.ln[:], [], [v("LNI")])
    dma("S", T.WI[:], T.wt[:], [], [v("WI")])
    dma("Y", T.THI[0:8, :], T.th[:], [], [v("THI")])

    iota(v("pcI"), [[0, 1]], 0, 1)
    iota(v("MP"), [[0, 8], [1, 2], [0, 16]], 0, 0)
    iota(v("iw", 0, 16), [[1, 16]], 0, 0)
    iota(v("iw", 16, 32), [[16, 16]], 15, 0)
    iota(v("QC"), [[0, 16], [1, 16]], 0, 0)
    iota(v("mg"), [[1, 8], [0, 16]], 0, 0)
    iota(v("mq"), [[0, 8], [1, 16]], 0, 0)
    iota(v("mm"), [[1, 128]], 0, 0)
    iota(v("cc"), [[1, 64]], 0, 0)
    iota(v("bcI"), [[16, 4], [0, 16]], 0, 0)
    iota(v("f2", 0, 16), [[16, 16]], W + 2, 0)
    ts(v("pmI"), v("pcI"), 15, OP.bitwise_and)
    ts(v("p4I"), v("pcI"), 4, OP.arith_shift_right)
    ts(v("btI"), v("p4I"), 1, OP.bitwise_and)
    for a, b in (("pcF", "pcI"), ("pmF", "pmI"), ("p4F", "p4I"), ("btF", "btI")):
        cp(v(a), v(b))
    ts(v("MP"), v("MP"), v("btF"), OP.is_equal)
    cp(v("bcA"), v("iw", 0, 16))
    cp(v("bc15"), v("iw", 16, 32))

    def conv(src, dst):
        act(v("CIN2", 0, 240), v(src, 16, 256))
        act(v("CIN2", 240, 256), v(src, 0, 16))
        tr(v("CT1"), v(src))
        tr(v("CT2"), v("CIN2"))
        act(v("pb6", 16, 256), v("CT2", 0, 240))
        act(v("pb6", 0, 16), v("CT2", 240, 256))
        tt(v("pb5", 0, 256), v("CT1"), v("pb6", 0, 256), OP.subtract)
        tt(v("m9"), v("pb5", 0, 256), v("MP"), OP.mult)
        tt(v(dst), v("m9"), v("pb6", 0, 256), OP.add)

    ts(v("m1"), v("IV"), 4096.0, OP.mult)
    tt(v("VCA"), v("m1"), v("IC"), OP.add)
    conv("VCA", "VCB")
    cp(v("iw"), v("VCB"))
    ts(v("IV"), v("iw"), 12, OP.arith_shift_right)
    cp(v("LST", 0, 256), v("IV"))
    ts(v("IC"), v("iw"), 4095, OP.bitwise_and)
    cp(v("LST", 256, 511), v("IV", 1, 256))
    cp(v("LST", 511, 512), v("IV", 255, 256))
    cp(v("LST", 512, 768), v("IC"))

    def consts1():
        cp(v("V"), v("IV"))
        cp(v("C"), v("IC"))
        cp(v("N", 0, 255), v("V", 1, 256))
        cp(v("N", 255, 256), v("V", 255, 256))
        ts(v("V0"), v("V", 0, 256, 16), 2.0, OP.add)
        ts(v("DG"), v("QC"), v("pmF"), OP.is_equal)
        ts(v("RS"), v("QC"), 0.0, OP.is_gt)
        op("V", lambda e: e.tensor_scalar(T.G8[0:8, :], T.mg[0:8, :], v("pcF", p=8)[0], None, OP.is_equal), [v("mg"), v("pcF")], [v("G8")])
        op("V", lambda e: e.tensor_copy(T.LNF[0:8, :], T.LNI[0:8, :]), [v("LNI")], [v("LNF")])
        op("V", lambda e: e.tensor_copy(T.THF[0:8, 0:1], T.THI[0:8, :]), [v("THI")], [v("THF")])
        op("T", lambda e: e.matmul(T.pb0[:, 0:256], T.G8[0:8, :], T.LNF[0:8, :], True, True), [v("G8"), v("LNF")], [v("pb0", 0, 256)])
        op("T", lambda e: e.matmul(T.pb1[:, 0:1], T.G8[0:8, :], T.THF[0:8, 0:1], True, True), [v("G8"), v("THF")], [v("pb1", 0, 1)])
        cp(v("pb7", 0, 256), v("QC"))
        tt(v("f1"), v("pb0", 0, 256), v("DG"), OP.mult)
        scan(v("f2"), v("RS"), v("f1"), OP.mult, OP.add)
        cp(v("nn"), last("f2"))
        ts(v("thm"), v("pb1", 0, 1), 0.5, OP.mult, -8192.0, OP.add)
        cp(v("lim"), v("thm"))
        limits()
        ts(v("Ident"), v("mm"), v("pcF"), OP.is_equal)
        for nm, c in (("In1", -1.0), ("In2", -2.0), ("Ibig", BIG), ("Im256", -256.0), ("Im4k", -4096.0)):
            ts(v(nm), v("Ident"), c, OP.mult)
        fill(v("ones"), 1.0)
        ts(v("IdF"), v("mm"), v("pcF"), OP.is_equal)

    def consts2():
        ts(v("blkF"), v("mg"), v("p4F"), OP.is_equal)
        tt(v("f1", 0, 128), v("mq"), v("blkF"), OP.mult)
        ts(v("f1", 128, 256), v("blkF"), -99.0, OP.mult, 99.0, OP.add)
        tt(v("mq"), v("f1", 0, 128), v("f1", 128, 256), OP.add)
        ts(v("e1"), v("pcF"), 0.0, OP.is_equal)
        ts(v("e2"), v("pcF"), 1.0, OP.is_equal, 3840.0, OP.mult)
        ts(v("ws"), v("pcF"), 2.0, OP.is_equal, -BIG, OP.mult)
        tt(v("e2"), v("e2"), v("ws"), OP.add)
        ts(v("CR"), v("cc"), v("e1"), OP.mult, v("e2"), OP.add)
        for q in range(16):
            ts(v("LQ1", q * 128, q * 128 + 128), v("mq"), float(q), OP.is_equal)
        ts(v("LQk"), v("LQ1"), 4096.0, OP.mult)
        ts(v("bcY"), v("bcI"), v("pmF"), OP.add)
        ts(v("LQh"), v("LQ1"), -0.5, OP.mult)
        cp(v("wF"), v("WI"))
        ts(v("LW"), v("LQ1"), v("wF"), OP.mult)
        ts(v("LM"), v("QC"), v("pmF"), OP.is_le, -16384.0, OP.mult)
        ts(v("blk"), v("mg"), v("p4F"), OP.is_equal)
        ts(v("blk8k"), v("blk"), 8192.0, OP.mult)
        fill(v("onesF"), 1.0)
        ts(v("G8T"), v("mm", 0, 8), v("p4F"), OP.is_equal)

    ts(v("TR"), v("f2", 0, 16), v("pmF"), OP.add)

    def limits():
        ts(v("live"), v("nn"), 4.0, OP.is_ge)
        wide("ngB", "nn", 1.08, -3.29)
        wide("nlB", "nn", 1.0, -1.0)

    PP = v("pb7", 0, 256)

    def masks():
        act(v("m1"), PP, AF.Identity, scale=-8192.0, bias=131074.0)
        act(v("Pb"), PP)
        tt(v("Vg"), v("ngB"), PP, OP.is_ge)
        tt(v("VL"), v("nlB"), PP, OP.is_ge)
        tt(v("PW"), v("m1"), v("V"), OP.add)

    def dedupe(z, gap1, gap2):
        tt(v("Hx"), bc(v(z)), v("DG"), OP.mult)
        wide("zb", z)
        mm(v("pb4", 0, 256), v("blkF"), v("Hx"), True, True)
        gap1()
        tt(v("pb0", 0, 256), v("pb4", 0, 256), v("LM"), OP.add)
        cp(v("Ru"), v("pb4", 0, 256))
        tt(v("EQ", 0, 256), v("zb"), v("pb0", 0, 256), OP.is_equal)
        mm(v("pb5", 0, 256), v("blk8k"), v("EQ", 0, 256), True, False)
        at = 256
        for a in range(15):
            w = 240 - 16 * a
            ts(v("EQ", at, at + w), v("Ru", 256 - w, 256), v(z, a, a + 1), OP.is_equal)
            mm(v("pb5", 256 - w, 256), v("blk8k"), v("EQ", at, at + w), False, a == 14)
            at += w
        gap2()
        tt(v("f1"), v("pb5", 0, 256), v("DG"), OP.mult)
        scan(v("f2"), v("RS"), v("f1"), OP.mult, OP.add)
        tt(v("s5"), last("f2"), v("hp"), OP.add)
        tt(v("s8"), v("s5"), v("TR"), OP.min)
        ts(v("off16"), v("s8"), -2.0, OP.add)

    def names(yes):
        line(v("s6"), v(yes), -16384.0, 16384.0)
        tt(v("hp"), v("s6"), v("zL"), OP.add)

    def send(buf, dst_buf, dst_rank, lsem, asem):
        dst = T.cores[dst_rank]
        rid, pid, _se = topo.addr(dst)
        n = len(topo.engines(core, dst))

        def emit(rd, wr):
            wait("G", need("G", rd, wr))
            g.remote_dma(T[dst_buf][:], T[buf][:], T.sem[asem], T.sem[lsem], pid, rid, topo.mask(core, dst))
            record("Gr", bump("G", lsem, n), rd, wr)
        return add("G", emit, [v(buf)], [], 1.5, 3.0)

    def arrive(buf, asem, src_rank, sent):
        n = len(topo.engines(T.cores[src_rank], core))

        def emit(rd, wr):
            count[asem] = n
            clock[(asem, n)] = {}
            recs[buf] = [(0, 99999, (asem, n), "far", True)]
        add("F", emit, [], [v(buf)], 0.0, 1.0, [sent])

    def gv(c):
        (cp if c == 0 else act)(v("GV%d" % c), ind(v("X", 0, W), v("LST", 64 * c, 64 * c + 64)))

    gv(0)
    consts1()
    consts2()
    for t in range(ST):
        d = 1 + t % 3
        to, frm = (rank + d) % 4, (rank - d) % 4
        rL, rP, rY, rB = "rL%d" % t, "rP%d" % t, "rY%d" % t, "rB%d" % t
        lastt = t == ST - 1

        def gc(c):
            act(v("GC%d" % c), ind(v("X", 0, W), v("LST", 512 + 64 * c, 512 + 64 * c + 64)))

        def ss(c):
            tt(v("SS%d" % c), ind(v("X", 0, W), v("LST", 256 + 64 * c, 256 + 64 * c + 64)), v("GV%d" % c), OP.add)

        def dd(c):
            for k in range(2):
                b = "pb%d" % (2 * (c % 2) + k)
                mm(v(b), v("Ident"), v("SS%d" % c, 512 * k, 512 * k + 512), True, False)
                mm(v(b), v("In2"), v("GC%d" % c, 512 * k, 512 * k + 512), False, True)

        def ab(c):
            for k in range(2):
                act(v("AB%d" % (c % 2), 512 * k, 512 * k + 512), v("pb%d" % (2 * (c % 2) + k)), AF.Abs)

        def key(c):
            o = v("pb%d" % (4 + c % 2), 0, 64)
            mm(o, v("ones"), v("CR"), True, False)
            mm(o, v("Im256"), v("Pb", 64 * c, 64 * c + 64), False, False)
            mm(o, v("Ibig"), v("Vg", 64 * c, 64 * c + 64), False, False)
            for q in range(16):
                mm(o, v("LQk", 128 * q, 128 * q + 128), v("AB%d" % (c % 2), q, 1024, 16), False, q == 15)

        def pick_a(c):
            k = v("pb%d" % (4 + c % 2), 0, 64)
            lo, hi = 64 * c, 64 * c + 64
            a, b = 4 * c, 4 * c + 4
            scan(v("SK", lo, hi), v("RS", 0, 64), k, OP.mult, OP.max)
            ts(v("KA", a, b), last("SK", a, b), 63, OP.bitwise_and)
            ts(v("o16", a, b), v("KA", a, b), 16.0, OP.mult, v("pmF"), OP.add)
            cp(v("SYs", lo, hi), ind(v("GC%d" % c), v("o16", a, b)))
            act(v("KS", lo, hi), k)
            tt(v("GYs", lo, hi), ind(v("SS%d" % c), v("o16", a, b)), v("SYs", lo, hi), OP.subtract)
            ts(v("KB", a, b), last("SK", a, b), 3840, OP.bitwise_and)
            ts(v("kp2", a, b), v("KB", a, b), -1.0 / 256, OP.mult, 17.0, OP.add)
            ts(v("Y", lo, hi), v("GYs", lo, hi), 0.0, OP.max, 63.0, OP.min)

        def ee(c):
            lo, hi = 64 * c, 64 * c + 64
            tt(v("EE%d" % (c % 2)), ind(v("Y", lo, hi), v("bcY")), v("GV%d" % c), OP.max)
            tt(v("B3", lo, hi), ind(v("kp2"), v("bcA", 4 * c, 4 * c + 4)), v("Pb", lo, hi), OP.is_le)

        def ds(c):
            lo, hi = 64 * c, 64 * c + 64
            o = v("pb7", lo, hi)
            mm(o, v("Im4k"), v("VL", lo, hi), True, False)
            for q in range(16):
                mm(o, v("LQh", 128 * q, 128 * q + 128), v("GV%d" % c, q, 1024, 16), False, False)
            mm(o, v("Im4k"), v("B3", lo, hi), False, False)
            for q in range(16):
                mm(o, v("LQ1", 128 * q, 128 * q + 128), v("EE%d" % (c % 2), q, 1024, 16), False, q == 15)

        par[0] = 0
        sent = {}
        sent["R"] = send("VNC", rL, to, "lR", "aR%d" % t)
        masks()
        sent["P"] = send("Pb", rP, to, "lP", "aP%d" % t)
        for w in MEASURE.split():
            {"ss": ss, "gc": gc, "gv": gv, "dd": dd, "ab": ab, "ky": key, "pk": pick_a, "ee": ee, "ds": ds}[w[:2]](int(w[2:]))
        act(v("kb"), ind(v("SK"), v("bc15")))
        sent["Y"] = send("Y", rY, to, "lY", "aY%d" % t)
        for q in range(16):
            mm(v("pb6", 16, 32), v("LQh", 128 * q, 128 * q + 128), v("Y", q, 256, 16), q == 0, q == 15)
        for q in range(16):
            mm(v("pb6", 0, 16), v("LW", 128 * q, 128 * q + 128), v("Y", q, 256, 16), q == 0, q == 15)
        ts(v("Tl"), v("pb6", 16, 32), -1.0, OP.mult, v("lim"), OP.add)
        wide("TB", "Tl")
        OH, O15, KV, K2 = v("pb0", 256, 512), v("pb1", 0, 256), v("pb1", 256, 512), v("pb2", 0, 256)
        t1, SN, SC, PS = v("pb2", 256, 512), v("pb3", 0, 256), v("pb6", 0, 256), v("pb0", 0, 256)
        act(v("pb2", 256, 512), v("Pb"))
        tt(OH, v("kb"), v("KS"), OP.is_equal)
        tt(v("m2"), v("V"), OH, OP.mult)
        tt(v("m3"), v("N"), OH, OP.mult)
        scan(v("m4"), v("RS"), v("m2"), OP.mult, OP.add)
        scan(v("m5"), v("RS"), v("m3"), OP.mult, OP.add)
        ts(v("K37"), last("m4"), 37.0, OP.mult)
        kq = v("SB", 16, 32)
        line(kq, v("kp2"), -1.0, 17.0)
        cp(v("UI"), v("pb6", 0, 16))
        ts(v("UI"), v("UI"), 4095, OP.bitwise_and)
        tt(v("HI"), v("UI"), v("UI"), OP.mult)
        ts(v("HI"), v("HI"), 5, OP.arith_shift_right)
        line(v("SB", 32, 48), last("m5"), 1.0, 2.0)
        tt(v("HI"), v("HI"), v("K37"), OP.add)
        ts(v("HI"), v("HI"), 4095, OP.bitwise_and)
        ts(v("H2"), v("HI"), 2.0, OP.add)
        act(v("NKB"), ind(v("m5"), v("bc15")))
        act(v("VKB"), ind(v("m4"), v("bc15")))
        ts(v("rest"), v("kp2"), 17.0, OP.is_equal)
        F = v("pb0", 0, 256)
        tt(F, v("TB"), v("pb7", 0, 256), OP.is_ge)
        tt(v("m1"), F, v("PW"), OP.mult)
        scan(v("SM"), v("RS"), v("m1"), OP.mult, OP.max)
        ts(v("close"), last("SM"), 0.0, OP.is_gt)
        ts(v("MX"), last("SM"), 13, OP.arith_shift_right)
        ts(v("VM"), last("SM"), 8191, OP.bitwise_and)
        tt(v("s1"), kq, v("MX"), OP.subtract)
        tt(v("SB", 0, 16), v("s1"), v("close"), OP.mult)
        sent["B"] = send("SB", rB, to, "lB", "aB%d" % t)
        tt(v("grow"), v("live"), v("close"), OP.subtract)
        tt(v("zL"), v("H2"), v("grow"), OP.mult)
        names("grow")
        wide("s6B", "grow", 16.0, -1.0)
        tt(v("x"), v("zL"), v("VM"), OP.add)

        def gap1():
            wide("xB", "x", 1.0, -2.0)
            tt(v("s3"), v("nn"), v("grow"), OP.add)
            ts(v("s3"), v("s3"), 16.0, OP.min)
            tt(O15, v("s6B"), v("pb2", 256, 512), OP.is_equal)
            tt(v("nn"), v("s3"), v("SB", 0, 16), OP.subtract)
            act(KV, O15, AF.Identity, scale=-1.0, bias=1.0)
            act(v("KVs"), O15, AF.Identity, scale=-1.0, bias=1.0)
            op("V", lambda e: e.tensor_reduce(v("cs1")[0], v("close")[0], AxisListType.X, OP.add), [v("close")], [v("cs1")])
            tt(v("MXe"), v("MX"), v("grow"), OP.add)

        def gap2():
            mm(v("pb6", 0, 1), v("onesF"), v("cs1"), True, True)
            tt(K2, v("KVs"), OH, OP.subtract)
            tt(v("m7"), v("xB"), O15, OP.mult)
            tt(t1, v("V"), KV, OP.mult)
            tt(v("V"), t1, v("m7"), OP.add)

        dedupe("zL", gap1, gap2)
        cp(ind(v("X"), v("off16")), v("Y"))
        if not lastt:
            tt(v("m8"), v("xB"), OH, OP.mult)
            tt(v("m9"), v("NKB"), O15, OP.mult)
            mm(SN, v("IdF"), v("m8"), True, False)
            mm(SN, v("IdF"), v("m9"), False, False)
        tt(v("nC"), v("VKB"), O15, OP.mult)
        cp(v("cI"), v("pb6", 0, 1))
        ts(v("cI"), v("cI"), 31, OP.bitwise_and)
        ts(v("lim"), v("cI"), 0.5, OP.mult, v("thm"), OP.add)
        mm(SC, v("IdF"), v("m3"), True, False)
        mm(SC, v("IdF"), v("nC"), False, False)
        for m, b in (("R", rL), ("P", rP), ("Y", rY), ("B", rB)):
            arrive(b, "a%s%d" % (m, t), frm, sent[m])
        par[0] = 1
        e_, k_, n_ = v(rB, 0, 16), v(rB, 16, 32), v(rB, 32, 48)
        act(v("s4"), k_, AF.Sign)
        tt(v("s1"), e_, v("nn"), OP.is_gt)
        ts(v("s7"), v("nn"), 1.0, OP.is_ge)
        tt(v("s9"), v("s7"), v("s4"), OP.mult)
        tt(v("Z0"), v("V0"), v("s9"), OP.mult)
        tt(v("Z1"), n_, v("Z0"), OP.subtract)
        tt(v("take"), v("s1"), v("rest"), OP.mult)
        tt(v("Z1"), v("Z1"), v("take"), OP.mult)
        tt(v("zL"), v("Z0"), v("Z1"), OP.add)
        tt(v("has"), v("s9"), v("take"), OP.max)
        names("has")
        tt(v("s2"), n_, v("V0"), OP.subtract)
        tt(v("s3"), e_, v("nn"), OP.subtract)
        wide("TKb", "take")
        act(v("pb1", 0, 256), v("TKb"))
        act(v("pb1", 256, 512), v("TKb"), AF.Identity, scale=-1.0, bias=1.0)
        TP, NT = v("pb1", 0, 256), v("pb1", 256, 512)
        tt(v("s2"), v("s2"), v("take"), OP.mult)
        tt(v("s3"), v("s3"), v("take"), OP.mult)
        tt(v("V0"), v("V0"), v("s2"), OP.add)
        tt(v("nn"), v("nn"), v("s3"), OP.add)
        ts(v("z16"), v("V0"), -2.0, OP.add)

        def take(k, acc):
            own = v("VNC", 256 * k, 256 * k + 256)
            a, b = v("m%d" % (2 * k)), v("m%d" % (2 * k + 1))
            tt(a, own, v("pb2", 0, 256), OP.mult)
            tt(b, v(rL, 256 * k, 256 * k + 256), TP, OP.mult)
            mm(acc, v("IdF"), a, False, False)
            mm(acc, v("IdF"), b, False, True)
            act(own, acc)
            if not lastt:
                cp(v("LST", 256 * k, 256 * k + 256), acc)

        def gap3():
            tt(t1, v("V"), NT, OP.mult)
            tt(v("m1"), v(rL, 0, 256), TP, OP.mult)
            tt(v("V"), t1, v("m1"), OP.add)
            if not lastt:
                cp(v("LST", 0, 256), v("V"))
            tt(K2, K2, v("TKb"), OP.subtract)
            tt(v("s2"), v("take"), k_, OP.mult)
            line(v("s3"), v("take"), 16.0, 0.0)
            tt(v("MXe"), v("MXe"), v("s2"), OP.add)
            tt(v("kqe"), kq, v("s3"), OP.add)
            wide("MXB", "MXe")
            wide("kqB", "kqe")
            line(v("kthB"), v("kqB"), -1.0, 15.0)
            line(v("mthB"), v("MXB"), -1.0, 16.0)
            limits()

        def gap4():
            tt(v("Pa"), v("Pb"), NT, OP.mult)
            tt(v("Pr"), v(rP), TP, OP.mult)
            tt(v("BL"), ind(v("X", 0, W), v("z16")), v(rY), OP.add)
            ts(v("BL2"), v("BL"), 0.5, OP.mult, 159.75, OP.add)
            ts(v("BL"), v("BL2"), -160.0, OP.add)
            if not lastt:
                take(1, SN)
            take(2, SC)

        dedupe("zL", gap3, gap4)
        cp(ind(v("X"), v("off16")), v("BL"))
        if lastt:
            dma("Y", T.yx[:, 0:half], T.X[:, 0:half], [v("X", 0, half)], [])
            dma("S", T.yx[:, half:W], T.X[:, half:W], [v("X", half, W)], [])
        else:
            gv(0)
        mm(PS, v("Ident"), v("Pa"), True, False)
        mm(PS, v("Ident"), v("Pr"), False, True)
        ga, gb = v("pb2", 0, 256), v("pb2", 256, 512)
        tt(ga, v("kthB"), PS, OP.is_lt)
        tt(gb, v("mthB"), PS, OP.is_le)
        tt(v("g1"), v("MXB"), ga, OP.mult)
        tt(v("g2"), v("kqB"), gb, OP.mult)
        mm(PP, v("Ident"), v("Pa"), True, False)
        mm(PP, v("Ident"), v("Pr"), False, False)
        mm(PP, v("Ident"), v("g1"), False, False)
        mm(PP, v("In1"), v("g2"), False, True)

    tt(v("Hx"), bc(v("nn")), v("DG"), OP.mult)
    op("T", lambda e: e.matmul(T.pb4[0:8, 0:256], T.G8T[:], v("Hx")[0], True, True), [v("G8T"), v("Hx")], [v("pb4", 0, 256)])
    ts(v("m7"), v("V"), 4096.0, OP.mult)
    VC = v("pb2", 0, 256)
    tt(VC, v("m7"), v("C"), OP.add)
    tt(v("pb3", 0, 256), v("nlB"), PP, OP.is_ge)
    line(v("m6"), v("pb3", 0, 256), -100.0, 100.0)
    tt(v("Pa"), PP, v("m6"), OP.add)
    op("V", lambda e: e.tensor_copy(T.LNF[0:8, :], T.pb4[0:8, 0:256]), [v("pb4", 0, 256)], [v("LNF")])
    dma("Y", T.yn[:], T.LNF[0:8, :], [v("LNF")], [])
    for p in range(16):
        b, pr, sn = v(("g1", "g2", "Pr")[p % 3]), v("m%d" % (2 + p % 3)), ("m5", "m7", "m8")[p % 3]
        ts(b, v("Pa"), float(p), OP.is_equal)
        tt(pr, b, VC, OP.mult)
        scan(v(sn), v("RS"), pr, OP.mult, OP.add)
        act(v("SO", p, 256, 16), last(sn))
    conv("SO", "VCB")
    cp(v("iw"), v("VCB"))
    ts(v("IV"), v("iw"), 12, OP.arith_shift_right)
    ts(v("IC"), v("iw"), 4095, OP.bitwise_and)
    cp(v("V"), v("IV"))
    dma("Y", T.yv[:], v("V")[0], [v("V")], [])
    cp(v("C"), v("IC"))
    dma("S", T.yc[:], v("C")[0], [v("C")], [])
    for i in order():
        OPS[i][1](OPS[i][2], OPS[i][3])
    for s in sorted(count):
        if known["G"].get(s, 0) < count[s]:
            g.wait_ge(T.sem[s], count[s])
